import numpy as np, ml_dtypes
CORES = [23,119,17,113]
N = 4
BF = ml_dtypes.bfloat16
def gentries(a):
    return np.ascontiguousarray(a.reshape(8, 16, -1).transpose(0, 2, 1)).reshape(8, -1)
def gtable(e):
    e = np.asarray(e); return np.ascontiguousarray(e.reshape(8, -1, 16).transpose(0, 2, 1)).reshape(128, -1).astype(np.int32)
W, R, NR, TV = 4096, 16, 256, 5
K = R * NR; NONE = W - 1; SH = (N, 8, R, NR)
def hsh(a, b):
    return (((a * b) >> 5) + 37 * a + b) & (W - 1)
def pack(x, y, g, a, b, t):
    o = {"xt": np.ascontiguousarray(x.reshape(N, 128, W)).astype(np.float32).astype(BF), "yv": np.ascontiguousarray(y.reshape(N, 128, TV * NR)).astype(np.float32).astype(BF)}
    for k, v in (("gl", g), ("al", a), ("bl", b), ("th", t)): o[k] = np.stack([gtable(w.reshape(8, -1)) for w in v])
    return o
def robots(rng, share, mem):
    g = np.where(rng.random(SH) < share, rng.integers(0, NONE, SH), NONE); keep = rng.random(SH) < mem
    return g, np.where(keep, rng.integers(0, NONE, SH), NONE), np.where(keep, rng.integers(0, NONE, SH), NONE)
def pool(rng, goals, m):
    a = rng.permutation(NONE)[:64]; a[0] = 64; a[1] = 128
    lut = np.zeros(W, bool); lut[goals] = True
    i, j = np.nonzero(lut[hsh(a[:, None], np.arange(NONE)[None, :])]); s = rng.integers(0, len(i), m)
    return a[i[s]], j[s]
def halves(rng, x, y, q, e):
    near = np.zeros(W, bool); near[rng.permutation(NONE)[:W // 2]] = True
    x[q, e] = np.where(near[None, :], rng.integers(0, 64, (16, W)), rng.integers(128, 256, (16, W)))
    y[q, e, :, 0] = rng.integers(0, 64, (16, NR))
    return near
def pairs(rng, near):
    far = rng.permutation(np.nonzero(~near[:NONE])[0]); a = far[:128]
    i, j = np.nonzero(near[hsh(a[:, None], far[None, :])]); s = rng.permutation(len(i))
    u, v = a[i[s]], far[j[s]]
    return u, v, hsh(u, v)
def setup_inputs(rng):
    x = rng.integers(0, 256, (N, 8, 16, W)); y = rng.integers(0, 256, (N, 8, 16, TV, NR))
    g, a, b = robots(rng, rng.choice(np.array([0.3, 0.6, 0.9, 1.0]), (N, 8, 1, NR)), 0.4)
    return pack(x, y, g, a, b, rng.integers(900, 1700, SH))
def setup_inputs_clash(rng):
    x = rng.integers(0, 256, (N, 8, 16, W)); y = rng.integers(0, 256, (N, 8, 16, TV, NR)); g, a, b = robots(rng, 1.0, 0.3)
    for q in range(N):
        for e in range(8):
            goals = np.concatenate([np.array([0, W - 2]), rng.integers(1, W - 2, 2)]); c = rng.integers(0, 256, 16)
            x[q, e][:, goals] = c[:, None]; y[q, e][:, 0, :] = c[:, None]
            u, v = pool(rng, goals, (R // 2) * NR)
            g[q, e, 0::2] = u.reshape(R // 2, NR); g[q, e, 1::2] = v.reshape(R // 2, NR)
    g = np.where((rng.random((N, 8, 1, NR)) < 0.3) | (rng.random(SH) < 0.1), NONE, g)
    for q in range(N):
        for s, e in enumerate(rng.permutation(8)[:2]):
            u, v, n = pairs(rng, halves(rng, x, y, q, e))
            if s == 0:
                w = np.nonzero(n == n[0])[0]; i = w[rng.integers(0, len(w), K // 2)]
            else:
                i = rng.integers(0, len(n), K // 2); i[:NR] = rng.permutation(np.unique(n, return_index=True)[1])[:NR]
            g[q, e, 0::2] = u[i].reshape(R // 2, NR); g[q, e, 1::2] = v[i].reshape(R // 2, NR)
    return pack(x, y, g, a, b, rng.integers(900, 1700, SH))
def setup_inputs_ties(rng):
    s = rng.integers(0, 2, (N, 8, 1, 1)) * 3 + 1
    x = 100 + s * rng.integers(0, 8, (N, 8, 16, W)); y = 100 + s[..., None] * rng.integers(0, 8, (N, 8, 16, TV, NR))
    g, a, b = robots(rng, rng.choice(np.array([0.4, 0.7, 1.0]), (N, 8, 1, NR)), 0.6)
    return pack(x, y, g, a, b, np.where(s == 1, rng.integers(0, 60, SH), rng.integers(60, 200, SH)))
def setup_inputs_corners(rng):
    x = rng.integers(0, 256, (N, 8, 16, W)); y = rng.integers(0, 256, (N, 8, 16, TV, NR)); g, a, b = robots(rng, 1.0, 1.0)
    kd = rng.integers(0, 11, (N, 8, 1, NR)); k = np.arange(R)[None, None, :, None]
    none = g.copy()
    for q in range(N):
        for e in range(8):
            u, v = pool(rng, np.array([NONE]), (R // 2) * NR)
            none[q, e, 0::2] = u.reshape(R // 2, NR); none[q, e, 1::2] = v.reshape(R // 2, NR)
    g = np.where(kd == 6, g[:, :, :1], np.where(kd == 8, none, np.where((kd == 10) & (k % 2 == 0), 0, g)))
    full = (kd == 1) | ((kd == 2) & (k % 2 == 0)) | ((kd == 3) & (k % 2 == 1)) | ((kd == 4) & (k == R - 1)) | ((kd == 5) & (k == 0)) | (kd == 6) | ((kd == 7) & (k % 4 < 2)) | (kd == 8) | ((kd == 9) & (rng.random(SH) < 0.5)) | (kd == 10)
    g = np.where(full, g, NONE)
    a = np.where((kd == 9) | ((kd == 10) & (rng.random(SH) < 0.5)), NONE, a); b = np.where(kd == 7, NONE, b)
    a = np.where(rng.random(SH) < 0.05, rng.choice(np.array([0, W - 2]), SH), a)
    t = rng.choice(np.array([0, 4080, 1300, 1400]), SH, p=[0.3, 0.2, 0.25, 0.25])
    for q in range(N):
        for s, e in enumerate(rng.permutation(8)[:2]):
            near = halves(rng, x, y, q, e); far = np.nonzero(~near[:NONE])[0]
            second = (np.arange(R)[:, None] + rng.integers(0, 2, NR)[None, :]) % 2 == 0
            if s == 0:
                a[q, e] = rng.integers(0, NONE, (R, NR)); t[q, e] = rng.integers(0, 1000, (R, NR))
            else:
                far = far[near[hsh(NONE, far)]]; w = rng.random((R, NR)) < 0.5
                a[q, e] = np.where(w, NONE, a[q, e]); t[q, e] = np.where(w, t[q, e], 4080)
            g[q, e] = np.where(second, far[rng.integers(0, len(far), (R, NR))], NONE)
    return pack(x, y, g, a, b, t)
def setup_inputs_ends(rng):
    v = 255 * rng.integers(0, 2, (N, 1, 1, 1)); e = rng.integers(0, 4, (N, 8, 1, W))
    x = np.where(e == 0, 0, np.where(e == 1, 255, 255 * rng.integers(0, 2, (N, 8, 16, W))))
    near = (rng.random((N, 8, 1, W)) < 0.25) & (np.arange(16)[None, None, :, None] == rng.integers(0, 16, (N, 8, 1, W)))
    x = np.where(near, np.abs(x - 1), x)
    x[..., 0] = v[..., 0]; x[..., W - 2] = v[..., 0]; x[..., W - 74] = 255 - v[..., 0]
    e = rng.integers(0, 3, (N, 8, 1, TV, NR)); y = np.where(e == 0, 0, np.where(e == 1, 255, 255 * rng.integers(0, 2, (N, 8, 16, TV, NR))))
    S = np.array([0, 1, int(rng.integers(2, NR - 2)), NR - 2, NR - 1])
    k = np.arange(R)[None, None, :, None]
    ty = rng.choice(np.array([0, 1, 2]), (N, 8, 1, NR), p=[0.6, 0.3, 0.1])
    ty[..., S] = 1
    g = np.where(ty == 0, rng.choice(np.array([0, NONE]), SH), np.where(ty == 1, np.where(k % 2 == 0, W - 2, 0), np.where(rng.random(SH) < 0.3, NONE, rng.integers(0, NONE, SH))))
    a = rng.choice(np.array([0, NONE, W - 2]), SH, p=[0.45, 0.45, 0.1]); b = rng.choice(np.array([0, NONE, W - 2]), SH, p=[0.45, 0.45, 0.1])
    t = rng.choice(np.array([0, 4080, 4079, 1]), SH, p=[0.4, 0.4, 0.1, 0.1])
    far = np.roll(v, -1, axis=0)
    for i in S:
        y[:, :, :, 0, i] = 255 - v[..., 0]; y[:, :, :, 1, i] = 255 - far[..., 0]
        t[:, :, :, i] = 4080 - 4 * R - (np.arange(R)[None, None, :] // 2) % 2
    return pack(x, y, g, a, b, t)
def setup_inputs_spread(rng):
    x = np.minimum((np.exp2(8 * rng.random((N, 8, 1, W))) * rng.random((N, 8, 16, W))).astype(np.int64), 255)
    y = np.minimum((np.exp2(8 * rng.random((N, 8, 1, TV, NR))) * rng.random((N, 8, 16, TV, NR))).astype(np.int64), 255)
    g, a, b = robots(rng, rng.random((N, 8, 1, NR)), rng.random((N, 8, 1, NR)))
    few = rng.random((N, 8, 1, NR)) < 0.5
    g = np.where(few & (g != NONE), np.minimum((NONE * rng.random(SH) ** 6).astype(np.int64), NONE - 1), g)
    t = np.minimum(np.exp2(12 * rng.random(SH)).astype(np.int64) - 1, 4080)
    return pack(x, y, g, a, b, t)
def check_inputs(d):
    bad = []
    for k, hi in (("xt", 255), ("yv", 255), ("gl", NONE), ("al", NONE), ("bl", NONE), ("th", 4080)):
        v = np.asarray(d[k]).astype(np.float64)
        if not (np.all(v >= 0) and np.all(v <= hi)): bad.append("range of " + k)
        elif np.any(v != np.floor(v)): bad.append("whole numbers of " + k)
    return bad
def reference(xt, yv, gl, al, bl, th):
    x = xt.astype(np.float32).astype(np.int32).reshape(N, 8, 16, W); y = yv.astype(np.float32).astype(np.int32).reshape(N, 8, 16, TV, NR)
    g, a, b, h = [np.stack([gentries(v) for v in w]).astype(np.int32).reshape(N, 8, R, NR) for w in (gl, al, bl, th)]
    c = np.zeros((N, NR), np.int32); row = np.arange(R)[None, :, None]; rob = np.arange(NR)[None, :]
    for t in range(TV):
        for r in range(N):
            q = (r + t) % N; G, A, B = g[r].copy(), a[r].copy(), b[r].copy()
            G1 = np.roll(G, -1, axis=1); n = hsh(G, G1); view = y[r][:, :, t][:, :, None, :]
            xg = np.take_along_axis(x[q], G.reshape(8, 1, K), 2); xn = np.take_along_axis(x[q], n.reshape(8, 1, K), 2)
            dg = np.add.reduce(np.abs(xg.reshape(8, 16, R, NR) - view), axis=1); dn = np.add.reduce(np.abs(xn.reshape(8, 16, R, NR) - view), axis=1)
            dg1 = np.roll(dg, -1, axis=1); full = G != NONE; full1 = np.roll(full, -1, axis=1)
            opens = full & (A != NONE) & ~full1 & (dg > h[r] + c[r][None, None, :])
            opened = np.roll(opens, 1, axis=1)
            merge = full & full1 & ~np.roll(opens, -1, axis=1) & ((row + t) % 2 == 0) & (n != NONE) & (dn < np.minimum(dg, dg1))
            gone = np.roll(merge, 1, axis=1)
            take = ~full & ~opened & full1 & (n != NONE) & (dn < dg1)
            some = np.any(merge, axis=1); low = np.argmax(merge, axis=1)
            i0 = low * NR + rob; i1 = ((low + 1) % R) * NR + rob
            val = (np.take_along_axis(xg, i0[:, None, :], 2) + np.take_along_axis(xg, i1[:, None, :], 2)) >> 1
            goal = np.take_along_axis(n.reshape(8, K), i0, 1)
            for e in range(8):
                w = np.nonzero(some[e])[0]; u, first = np.unique(goal[e][w], return_index=True)
                x[q, e][:, u] = val[e][:, w[first]]
            clear = opens | opened | gone | take
            g[r] = np.where(opens, A, np.where(opened, np.roll(B, 1, axis=1), np.where(merge | take, n, np.where(gone, NONE, G))))
            na = np.where(merge, G, np.where(clear, NONE, A)); nb = np.where(merge, G1, np.where(clear, NONE, B))
            a[r] = na; b[r] = nb; c[r] = np.add.reduce(merge.astype(np.int32), axis=(0, 1))
    o = [np.stack([gtable(v.reshape(8, -1)) for v in w]).astype(np.float32) for w in (g, a, b)]
    return {"og": o[0], "oa": o[1], "ob": o[2], "ox": x.reshape(N, 128, W).astype(np.float32).astype(BF)}

@@ -1,0 +1,437 @@
+import numpy as np
+from concourse.mybir import dt, AluOpType as Op, ActivationFunctionType as Fn
+
+VIS = 5
+H = 65536.0
+F32, BF, I32, U16 = "float32", "bfloat16", "int32", "uint16"
+SCRATCH = {}
+
+
+def _declare(where, dtype, names):
+    for name, shape in names.items():
+        SCRATCH[name] = (where, [128] + (list(shape) if isinstance(shape, tuple) else [shape]), dtype)
+
+
+_declare("sbuf", BF, {
+    "TAB": 4352, "XLAST": 16, "YV": 1280, "TH": 512, "XRM": 2048, "XRO": 2048, "XRN": 2048, "MX": 6144, "EQ": 2176,
+    "SEL2": 2048, "SELN": 2048, "DS": 2048, "WE": 1024, "TMPC": 128, "IDX": 16, "ID": 128, "NID": 128, "N16": 128,
+    "NH": 128, "PH": 128, "N4K": 128, "MOD16": 128, "BLK": 128, "TRI": 128, "ZER": 128, "ONES": 256, "FB": 256, "EB": 256,
+    "EA": 256, "HE2": 256, "OPB": 256, "TKO": 128, "MGB": 128, "FMB": 128, "NOM": 16, "OUTS": 256, "CS": 64,
+    "VR0": 2048, "VR1": 2048})
+_declare("sbuf", I32, {
+    "IOTA": 4096, "LG": (16, 16), "LA": (16, 16), "LBM": (16, 16), "LT": (16, 16), "THI": 512, "PM": 128, "PR": 128,
+    "MC": 128, "TMPA": 128, "TMPB": 128, "C16": 16, "P15": 16, "PI": 256, "SH": 256, "S1": 256, "NHT": 256, "AH": 256,
+    "BH": 256, "VAL": 256, "AB_0": 256, "AS": 1280})
+_declare("sbuf", F32, {
+    "DUMP": 16, "N37F": 128, "N1F": 128, "GF": 256, "GH": 256, "SELF": 128, "TS": 256, "DXS": 256, "DGN": 256, "MN": 128,
+    "MNG": 128, "MNA": 128, "G0": 256, "DNN": 128, "GN": 256, "FN": 128, "TR": 112, "GL": 16, "H1": 256, "SUM": 256,
+    "Q1": 16, "Q2": 16, "WO": 16, "AB0": 256, "G4": 128, "DAB": 128, "OG": (16, 16), "OA": (16, 16), "OB": (16, 16)})
+_declare("sbuf", U16, {"SELU": 128, "NU": 128, "GLU": 16, "GR": 256, "OFU": 32, "WOU": 16, "GU0": 256, "GS": 1024})
+PSUM = ["PV", "PL", "PG", "PN", "PT", "PM1", "VB1", "VB2"]
+_declare("psum", F32, {b: 512 for b in PSUM})
+for _t in range(1, VIS):
+    _declare("sbuf", U16, {"GU%d" % _t: 256})
+    _declare("sbuf", I32, {"AB_%d" % _t: 256})
+    _declare("sbuf", BF, {"CR%d" % _t: 16})
+for _t in range(1, VIS - 1):
+    _declare("sbuf", BF, {"VT%d" % _t: 256, "TH%d" % _t: 512})
+SEMAPHORES = (["qV", "qS", "qT", "qG", "lsem", "dx", "dxl", "dg", "da", "db", "dth", "dy", "do1", "do2", "do3", "do4"]
+              + ["vr%d" % t for t in range(VIS)]
+              + [n + "%d" % t for t in range(1, VIS) for n in ("ag", "ab", "ac")]
+              + [n + "%d" % t for t in range(1, VIS - 1) for n in ("av", "at")])
+
+
+def rank_program(g, core, T, topo):
+    rank = T.rank_of(core)
+    if rank is None:
+        return
+    eng = {"V": g.vector, "S": g.scalar, "T": g.tensor, "G": g, "Y": g.sync}
+    known = {q: {} for q in eng}
+    total = {}
+    clk = {}
+    log = {}
+
+    def take(q, tok):
+        k = known[q]
+        if k.get(tok[0], 0) >= tok[1]:
+            return
+        eng[q].wait_ge(T.sem[tok[0]], tok[1])
+        for s, n in clk.get(tok, {}).items():
+            if k.get(s, 0) < n:
+                k[s] = n
+        k[tok[0]] = tok[1]
+
+    def order(q, reads, writes, dma=False):
+        need = []
+        for w, regs in ((False, reads), (True, writes)):
+            for (b, a, e) in regs:
+                ps = b in PSUM
+                for (a2, e2, w2, q2, tok) in log.get(b, []):
+                    over = a < e2 and a2 < e
+                    same = q2 == q and not dma
+                    if ps and not same:
+                        need.append(tok)
+                    elif over and (w or w2):
+                        if same and not w2:
+                            continue
+                        if same and w and q == "T":
+                            continue
+                        need.append(tok)
+        need.sort(key=lambda x: -x[1])
+        for tok in need:
+            take(q, tok)
+
+    def note(q, reads, writes, tok):
+        for (b, a, e) in writes:
+            log[b] = [x for x in log.get(b, []) if not (a <= x[0] and x[1] <= e)] + [(a, e, True, q, tok)]
+        for (b, a, e) in reads:
+            log[b] = [x for x in log.get(b, []) if not (a <= x[0] and x[1] <= e and not x[2] and x[3] == q)] + [(a, e, False, q, tok)]
+
+    def op(q, call, reads, writes):
+        order(q, reads, writes)
+        s = "q" + q
+        total[s] = total.get(s, 0) + 1
+        call().then_inc(T.sem[s], 1)
+        tok = (s, total[s])
+        clk[tok] = dict(known[q])
+        note(q, reads, writes, tok)
+
+    def dmas(q, sem, items):
+        n = 16 * len(items)
+        total[sem] = n
+        tok = (sem, n)
+        for (o, i, reads, writes) in items:
+            order(q, reads, writes, True)
+            eng[q].dma_start(o, i).then_inc(T.sem[sem], 16)
+        clk[tok] = dict(known[q])
+        for (o, i, reads, writes) in items:
+            note("dma" + sem, reads, writes, tok)
+
+    def R(r):
+        b, a, e = r
+        return T[b][:, a:e]
+
+    def tt(o, a, b, f):
+        op("V", lambda: g.vector.tensor_tensor(R(o), R(a), R(b), f), [a, b], [o])
+
+    def ts(o, a, s1, f1, s2=None, f2=None):
+        if f2 is None:
+            op("V", lambda: g.vector.tensor_scalar(R(o), R(a), s1, None, f1), [a], [o])
+        else:
+            op("V", lambda: g.vector.tensor_scalar(R(o), R(a), s1, s2, f1, f2), [a], [o])
+
+    def cp(o, a):
+        op("V", lambda: g.vector.tensor_copy(R(o), R(a)), [a], [o])
+
+    def act(o, a, scale=1.0, bias=0.0):
+        op("S", lambda: g.scalar.activation(R(o), R(a), Fn.Identity, bias=bias, scale=scale), [a], [o])
+
+    def mms(o_all, items, start, stop):
+        reads = []
+        for (o, l, r) in items:
+            reads += [l, r[0] if len(r) == 2 else r]
+
+        def call():
+            last = None
+            for k, (o, l, r) in enumerate(items):
+                if len(r) == 2:
+                    (b, a, e), s = r
+                    rhs = T[b][:, a + s:e:16]
+                else:
+                    rhs = R(r)
+                last = g.tensor.matmul(R(o), R(l), rhs, start and k == 0, stop and k == len(items) - 1)
+            return last
+        op("T", call, list(dict.fromkeys(reads)), [o_all])
+
+    def W(b, a=0, n=None):
+        return (b, a, a + (n if n is not None else int(np.prod(SCRATCH[b][1][1:])) - a))
+    mat = lambda b, s=0: (b, 128 * s, 128 * s + 128)
+    nxt = {0: [(0, 128, 128)], 128: [(0, 16, 112), (112, 0, 16)]}
+    prv = {128: [(0, 0, 128)], 0: [(0, 240, 16), (16, 128, 112)]}
+
+    def send(dst, out, src, sem):
+        c = T.cores[dst]
+        order("G", [src], [])
+        rid, pid = topo.addr(c)[:2]
+        g.remote_dma(R(out), R(src), T.sem[sem], T.sem.lsem, pid, rid, topo.mask(core, c))
+        total["lsem"] = total.get("lsem", 0) + len(topo.engines(core, c))
+
+    def arrives(frm, out, sem):
+        n = len(topo.engines(T.cores[frm], core))
+        total[sem] = n
+        note("remote", [], [out], (sem, n))
+
+    dmas("Y", "dg", [(T.LG[:], T.gl[:], [], [W("LG")])])
+    dmas("S", "dx", [(T.TAB[:, 0:4096], T.xt[:], [], [W("TAB", 0, 4096)])])
+    dmas("Y", "dy", [(T.YV[:], T.yv[:], [], [W("YV")])])
+    dmas("Y", "dth", [(T.LT[:], T.th[:], [], [W("LT")])])
+    dmas("Y", "da", [(T.LA[:], T.al[:], [], [W("LA")])])
+    dmas("Y", "db", [(T.LBM[:], T.bl[:], [], [W("LBM")])])
+    dmas("Y", "dxl", [(T.XLAST[:], T.xt[:, 4080:4096], [], [W("XLAST")])])
+    for t in range(1, VIS - 1):
+        arrives((rank - t) % 4, W("VT%d" % t), "av%d" % t)
+        arrives((rank - t) % 4, W("TH%d" % t), "at%d" % t)
+    for t in range(1, VIS):
+        arrives((rank - 1) % 4, W("GU%d" % t), "ag%d" % t)
+        arrives((rank - 1) % 4, W("AB_%d" % t), "ab%d" % t)
+        arrives((rank - 1) % 4, W("CR%d" % t), "ac%d" % t)
+    view = lambda t: W("YV", 256 * t, 256) if t in (0, VIS - 1) else W("VT%d" % t)
+    thr = lambda t: "TH" if t in (0, VIS - 1) else "TH%d" % t
+
+    def spread(t):
+        v, d = view(t), "VR%d" % (t % 2)
+        dmas("Y", "vr%d" % t, [(T[d][:, 256 * k:256 * k + 256], R(v), [v], [(d, 256 * k, 256 * k + 256)]) for k in range(8)])
+
+    def iota(b, pat, base, cm):
+        op("G", lambda: g.iota(T[b][:], pat, base, cm), [], [W(b)])
+    iota("PM", [[-1, 128]], 128, 1)
+    iota("PR", [[0, 128]], 0, 1)
+    iota("MC", [[1, 128]], 0, 0)
+    iota("C16", [[16, 16]], 0, 0)
+    for b, c in (("SELN", 0.0), ("SEL2", 0.0), ("ONES", 1.0), ("ZER", 0.0)):
+        op("V", lambda b=b, c=c: g.vector.memset(T[b][:], c), [], [W(b)])
+    ts(W("N37F"), W("PM"), 128.0, Op.is_equal, -37.0, Op.mult)
+    ts(W("N1F"), W("PM"), 128.0, Op.is_equal, -1.0, Op.mult)
+    for b, c in (("ID", 1.0), ("NID", -1.0), ("N4K", -4096.0), ("NH", -H), ("PH", H), ("N16", -16.0)):
+        ts(W(b), W("PM"), 128.0, Op.is_equal, c, Op.mult)
+    ts(W("TMPA"), W("PR"), 4, Op.arith_shift_right)
+    ts(W("TMPB"), W("MC"), 4, Op.arith_shift_right)
+    tt(W("BLK"), W("TMPA"), W("TMPB"), Op.is_equal)
+    for s in range(16):
+        z = (slice(None), slice(128 * s + s, 128 * s + 128, 16))
+        f = (slice(None), slice(s, 128, 16))
+        op("V", lambda z=z, f=f: g.vector.tensor_scalar(T.SELN[z], T.BLK[f], -1.0, None, Op.mult), [W("BLK")], [mat("SELN", s)])
+        op("S", lambda z=z, f=f: g.scalar.activation(T.SEL2[z], T.BLK[f], Fn.Identity, bias=0.0, scale=2.0), [W("BLK")], [mat("SEL2", s)])
+
+    ev = [(0, 0), (1, 128)]
+    for p, c in ev:
+        op("V", lambda p=p, c=c: g.vector.tensor_copy(T.GU0[:, c:c + 128], T.LG[:, p::2, :]), [W("LG")], [("GU0", c, c + 128)])
+        op("V", lambda p=p, c=c: g.vector.tensor_scalar(T.THI[:, c:c + 128], T.LT[:, p::2, :], 15, None, Op.bitwise_and), [W("LT")], [("THI", c, c + 128)])
+        op("V", lambda p=p, c=c: g.vector.tensor_scalar(T.THI[:, 256 + c:384 + c], T.LT[:, p::2, :], 4, None, Op.arith_shift_right), [W("LT")], [("THI", 256 + c, 384 + c)])
+    cp(W("TH"), W("THI"))
+    for t in range(1, VIS - 1):
+        send((rank + t) % 4, W("VT%d" % t), W("YV", 256 * t, 256), "av%d" % t)
+    for t in range(1, VIS - 1):
+        send((rank + t) % 4, W("TH%d" % t), W("TH"), "at%d" % t)
+    spread(0)
+    op("V", lambda: g.vector.memset(T.TAB[:, 4095:4096], 1024.0), [], [("TAB", 4095, 4096)])
+    iota("IOTA", [[1, 4096]], 0, 0)
+
+    def late():
+        for p, c in ev:
+            op("V", lambda p=p, c=c: g.vector.tensor_scalar(T.G0[:, c:c + 128], T.LA[:, p::2, :], -4096.0, 4095.0 * 4096 + 4095, Op.mult, Op.add), [W("LA")], [("G0", c, c + 128)])
+            op("V", lambda p=p, c=c: g.vector.tensor_copy(T.GN[:, c:c + 128], T.LBM[:, p::2, :]), [W("LBM")], [("GN", c, c + 128)])
+        tt(W("AB_0"), W("G0"), W("GN"), Op.subtract)
+
+    def later():
+        ts(W("TMPA"), W("PM"), 15, Op.bitwise_and)
+        ts(W("MOD16"), W("TMPA"), 0.0, Op.is_equal)
+        ts(W("TMPC"), W("PM"), 128.0, Op.is_lt)
+        tt(W("TRI"), W("TMPC"), W("BLK"), Op.mult)
+        for e in range(8):
+            ts(mat("WE", e), W("ID"), 256.0 * e, Op.mult)
+        ts(W("P15"), ("PR", 0, 16), 15, Op.bitwise_and)
+        tt(W("IDX"), W("C16"), W("P15"), Op.add)
+        ts(W("DUMP"), W("IDX"), 4096.0, Op.add)
+        op("V", lambda: g.vector.memset(T.DS[:], 0.0), [], [W("DS")])
+        for s in range(16):
+            op("V", lambda s=s: g.vector.tensor_copy(T.DS[:, 128 * s + s:128 * s + 128:16], T.ID[:, s:128:16]), [W("ID")], [mat("DS", s)])
+
+    def prepare(t):
+        v = view(t)
+        mms(W("PV"), [(("PV", 0, 256), W("ID"), v)], True, True)
+        mms(W("PV"), [(("PV", 256, 512), W("ID"), v)], True, True)
+        th, vr = thr(t), "VR%d" % (t % 2)
+        mms(("PT", 0, 256), [(("PT", 0, 256), W("NID"), (th, 0, 256)), (("PT", 0, 256), W("N16"), (th, 256, 512))], True, False)
+        mms(("PT", 0, 256), [(("PT", h, h + 128), mat("SELN", s), (W(vr), s)) for h in (0, 128) for s in range(16)], False, False)
+
+    def visit(t):
+        M = 0 if t % 2 == 0 else 128
+        O = 128 - M
+        hm = lambda b: (b, M, M + 128)
+        ho = lambda b: (b, O, O + 128)
+        gu = W("GU%d" % t)
+        last = t == VIS - 1
+
+        def gather(out, c, lst, lc):
+            op("S", lambda: g.scalar.activation(T[out][:, 1024 * c:1024 * c + 1024], T.TAB[:, 0:4096].indirect(T[lst][:, lc:lc + 64]), Fn.Copy),
+               [W("TAB", 0, 4096), (lst, lc, lc + 64)], [(out, 1024 * c, 1024 * c + 1024)])
+
+        def maxes(x, c, n):
+            for h in range(2):
+                a, z = 1024 * c + 512 * h, 1024 * n + 512 * h
+                tt(("MX", z, z + 512), (x, a, a + 512), W("PV"), Op.max)
+
+        def sums(x, c, n, bank, col, extra=()):
+            out = (bank, col, col + 64)
+            mms(out, [(out, mat("SELN", s), ((x, 1024 * c, 1024 * c + 1024), s)) for s in range(16)] + [(out, l, r) for l, r in extra], True, False)
+            mms(out, [(out, mat("SEL2", s), (("MX", 1024 * n, 1024 * n + 1024), s)) for s in range(16)], False, True)
+
+        gather("XRM", 0, gu[0], M)
+        gather("XRM", 1, gu[0], M + 64)
+        cp(W("GF"), gu)
+        mms(("PL", 0, 256), [(("PL", 0, 256), W("NID"), W("ONES")), (("PL", 0, 256), W("N37F"), W("GF"))]
+            + [(("PL", b + d, b + d + n), W("N1F"), ("GF", s, s + n)) for b in (0, 128) for d, s, n in nxt[b]], True, True)
+        ts(W("FB"), gu, 4095.0, Op.is_lt)
+        mms(("PL", 256, 384), [(("PL", 256, 384), W("N4K"), ho("FB"))], True, True)
+        for b in (0, 128):
+            for d, s, n in nxt[b]:
+                tt(("PI", b + d, b + d + n), ("GF", b + d, b + d + n), ("GF", s, s + n), Op.mult)
+        ts(W("SH"), W("PI"), 5, Op.arith_shift_right)
+        ts(W("GH"), gu, -1.0, Op.mult, 4095.0, Op.add)
+        tt(W("S1"), ("PL", 0, 256), W("SH"), Op.subtract)
+        ts(W("NHT"), W("S1"), 4095, Op.bitwise_and)
+        tt(("VB1", 0, 128), ("PL", 256, 384), ho("NHT"), Op.add)
+        tt(W("SELF"), ("VB1", 0, 128), ho("GH"), Op.max)
+        ts(W("SELU"), W("SELF"), -1.0, Op.mult, 4095.0, Op.add)
+        ts(W("NU"), hm("NHT"), -1.0, Op.mult, 4095.0, Op.add)
+        ts(W("EB"), gu, 4095.0, Op.is_ge)
+        ts(hm("HE2"), hm("EB"), 2 * H, Op.mult, H, Op.add)
+        if t == 0:
+            later()
+        gather("XRO", 0, "SELU", 0)
+        gather("XRO", 1, "SELU", 64)
+        maxes("XRM", 0, 0)
+        sums("XRM", 0, 0, "PG", M)
+        maxes("XRM", 1, 1)
+        sums("XRM", 1, 1, "PG", M + 64)
+        if t == 0:
+            late()
+        if t > 0:
+            mms(("PT", 0, 256), [(("PT", 16 * k, 16 * k + 16), W("NID"), W("CR%d" % t)) for k in range(16)], False, False)
+        ab = W("AB_%d" % t)
+        gather("XRN", 0, "NU", 0)
+        maxes("XRO", 0, 2)
+        sums("XRO", 0, 2, "PG", O, [(W("NH"), ("EB", O, O + 64))])
+        ts(W("EA"), ab, 4096.0, Op.is_lt)
+        mms(("PT", 0, 256), [(("PT", 0, 256), W("NH"), W("EB"))]
+            + [(("PT", b + d, b + d + n), W("PH"), ("EB", s, s + n)) for b in (0, 128) for d, s, n in nxt[b]]
+            + [(("PT", 0, 256), W("NH"), W("EA"))], False, True)
+        ts(W("AH"), ab, 12, Op.arith_shift_right)
+        ts(W("BH"), ab, 4095, Op.bitwise_and)
+        maxes("XRO", 1, 3)
+        sums("XRO", 1, 3, "PG", O + 64, [(W("NH"), ("EB", O + 64, O + 128))])
+        act(W("TS"), ("PT", 0, 256), -1.0, H)
+        act(ho("DXS"), ho("PG"))
+        gather("XRN", 1, "NU", 64)
+        act(W("G4"), hm("GH"), 4096.0)
+        maxes("XRN", 0, 4)
+        sums("XRN", 0, 4, "PN", 0)
+        tt(W("OPB"), ("PG", 0, 256), W("TS"), Op.is_gt)
+        mms(("PL", 0, 128), [(("PL", 0, 128), W("NH"), hm("EB"))] + [(("PL", d, d + n), W("NH"), ("OPB", s, s + n)) for d, s, n in nxt[M]], True, True)
+        mms(("PL", 128, 256), [(("PL", 128, 256), W("NH"), hm("FB"))] + [(("PL", 128 + d, 128 + d + n), W("NH"), ("OPB", s, s + n)) for d, s, n in prv[M]], True, True)
+        tt(hm("DGN"), hm("PG"), hm("HE2"), Op.subtract)
+        for d, s, n in nxt[O]:
+            tt(("VB2", d, d + n), ("PG", O + d, O + d + n), ("DGN", s, s + n), Op.is_lt)
+        for d, s, n in prv[O]:
+            tt(("TKO", d, d + n), ("VB2", d, d + n), ("OPB", s, s + n), Op.is_gt)
+        mms(("PL", 256, 512), [(("PL", 256, 512), W("ID"), W("ONES")), (("PL", 256, 512), W("NID"), W("OPB"))]
+            + [(("PL", 256 + b + d, 256 + b + d + n), W("NID"), ("OPB", s, s + n)) for b in (0, 128) for d, s, n in prv[b]]
+            + [(("PL", 256 + O, 384 + O), W("NID"), W("TKO"))], True, True)
+        tt(("VB1", 0, 256), ("PG", 0, 256), W("TS"), Op.is_gt)
+        for d, s, n in nxt[M]:
+            tt(("MN", d, d + n), ("PG", M + d, M + d + n), ("DXS", s, s + n), Op.min)
+        maxes("XRN", 1, 5)
+        sums("XRN", 1, 5, "PN", 64)
+        tt(("VB1", 256, 512), ("VB1", 0, 256), W("AH"), Op.mult)
+        tt(("VB1", 0, 256), ("VB1", 0, 256), W("BH"), Op.mult)
+        tt(W("MNG"), ("PL", 0, 128), W("MN"), Op.add)
+        tt(("VB2", 128, 256), ("PL", 128, 256), W("MN"), Op.add)
+        tt(W("MNA"), ("VB2", 128, 256), W("MNG"), Op.max)
+        tt(W("G0"), ("PL", 256, 512), W("GH"), Op.mult)
+        tt(W("G0"), ("VB1", 256, 512), W("G0"), Op.add)
+        for b in (0, 128):
+            for d, s, n in prv[b]:
+                tt(("G0", b + d, b + d + n), ("VB1", s, s + n), ("G0", b + d, b + d + n), Op.add)
+        tt(("VB2", 0, 128), W("TKO"), ho("NHT"), Op.mult)
+        tt(ho("G0"), ("VB2", 0, 128), ho("G0"), Op.add)
+        tt(W("DNN"), hm("NHT"), hm("G0"), Op.subtract)
+        tt(W("MGB"), ("PN", 0, 128), W("MNG"), Op.is_lt)
+        tt(("VB2", 256, 384), ("PN", 0, 128), W("MNA"), Op.is_lt)
+        tt(("VB2", 384, 512), ("PN", 0, 128), W("MNG"), Op.is_ge)
+        mms(("PM1", 0, 128), [(("PM1", 0, 128), W("N16"), W("MGB"))]
+            + [(("PM1", 16 * d, 128), W("ID"), ("MGB", 0, 128 - 16 * d)) for d in range(1, 8)], True, True)
+        if not last:
+            mms(("PT", 0, 16), [(("PT", 0, 16), W("MOD16"), ("MGB", 16 * e, 16 * e + 16)) for e in range(8)], True, True)
+            act(W("CS", 16 * t, 16), ("PT", 0, 16))
+        tt(("VB1", 0, 128), ("VB2", 256, 384), W("DNN"), Op.mult)
+        tt(hm("GN"), ("VB1", 0, 128), hm("G0"), Op.add)
+        for d, s, n in prv[O]:
+            tt(("GN", O + d, O + d + n), ("VB2", 384 + s - M, 384 + s - M + n), ("G0", O + d, O + d + n), Op.mult)
+        if not last:
+            ts(W("GS", 256 * t, 256), W("GN"), -1.0, Op.mult, 4095.0, Op.add)
+            send((rank + 1) % 4, W("GU%d" % (t + 1)), W("GS", 256 * t, 256), "ag%d" % (t + 1))
+            send((rank + 1) % 4, W("CR%d" % (t + 1)), W("CS", 16 * t, 16), "ac%d" % (t + 1))
+        ts(W("FMB"), ("PM1", 0, 128), -16.0, Op.is_equal)
+        sh = t % 2
+        for k in range(1 + sh):
+            o = ("PM1", 128 + 16 * k, 144 + 16 * k)
+            mms(o, [(o, W("ID"), W("IDX"))] + [(o, mat("WE", (e + k) % 8), ("FMB", 16 * e, 16 * e + 16)) for e in range(8)], True, True)
+        tt(W("FN"), W("FMB"), hm("NHT"), Op.mult)
+        tt(("TR", 0, 64), ("FN", 0, 64), ("FN", 64, 128), Op.add)
+        tt(("TR", 64, 96), ("TR", 0, 32), ("TR", 32, 64), Op.add)
+        tt(("TR", 96, 112), ("TR", 64, 80), ("TR", 80, 96), Op.add)
+        ts(W("GLU"), ("TR", 96, 112), -1.0, Op.mult, 4095.0, Op.add)
+        ts(W("GL"), ("TR", 96, 112), -1.0, Op.mult, 4095.0, Op.add)
+        op("V", lambda: g.vector.tensor_copy(T.GR[:], T.IOTA[:].indirect(T.GLU[:])), [W("IOTA"), W("GLU")], [W("GR")])
+        cp(("OFU", 0, 16 + 16 * sh), ("PM1", 128, 144 + 16 * sh))
+        op("S", lambda: g.scalar.activation(T.H1[:], T.XRM[:].indirect(T.OFU[:, 0:16]), Fn.Copy), [W("XRM"), ("OFU", 0, 16)], [W("H1")])
+        mms(("PT", 256, 512), [(("PT", 256, 512), W("ZER"), W("ONES"))], True, False)
+        at = 0
+        for c in range(16):
+            n = 256 - 16 * c
+            op("V", lambda c=c, at=at, n=n: g.vector.tensor_scalar(T.EQ[:, at:at + n], T.GR[:, 16 * c:256], T.GL[:, c:c + 1], None, Op.is_equal),
+               [W("GR"), W("GL")], [("EQ", at, at + n)])
+            it = [(("PT", 256 + 16 * c, 272 + 16 * c), W("TRI"), ("EQ", at, at + 16))]
+            if n > 16:
+                it.append((("PT", 272 + 16 * c, 512), W("BLK"), ("EQ", at + 16, at + n)))
+            mms(("PT", 256, 512), it, False, c == 15)
+            at += n
+        act(W("OUTS"), ("PT", 256, 512))
+        ts(W("NOM"), ("TR", 96, 112), 0.0, Op.is_equal)
+        mms(("PM1", 160, 176), [(("PM1", 160, 176), W("ID"), W("NOM"))]
+            + [(("PM1", 160, 176), mat("DS", s), (W("OUTS"), s)) for s in range(16)], True, True)
+        if not last:
+            prepare(t + 1)
+        op("V", lambda: g.vector.tensor_tensor(T.SUM[:], T.XRO[:].indirect(T.OFU[:, 16 * sh:16 * sh + 16]), T.H1[:], Op.add),
+           [W("XRO"), W("H1"), ("OFU", 16 * sh, 16 * sh + 16)], [W("SUM")])
+        ts(W("VAL"), W("SUM"), 0.5, Op.mult, -0.25, Op.add)
+        z = 256 * t
+        tt(W("AB0"), ("PL", 256, 512), ab, Op.mult)
+        for d, s, n in nxt[M]:
+            tt(("VB1", d, d + n), ("GH", s, s + n), ("FB", M + d, M + d + n), Op.mult)
+        tt(("VB1", 128, 256), ("VB1", 0, 128), W("G4"), Op.add)
+        tt(W("DAB"), ("VB1", 128, 256), hm("AB0"), Op.subtract)
+        tt(("VB1", 256, 384), ("VB2", 256, 384), W("DAB"), Op.mult)
+        tt(("AS", z + M, z + M + 128), ("VB1", 256, 384), hm("AB0"), Op.add)
+        for d, s, n in prv[O]:
+            tt(("AS", z + O + d, z + O + d + n), ("VB2", 384 + s - M, 384 + s - M + n), ("AB0", O + d, O + d + n), Op.mult)
+        if not last:
+            send((rank + 1) % 4, W("AB_%d" % (t + 1)), W("AS", z, 256), "ab%d" % (t + 1))
+        ts(W("Q1"), ("PM1", 160, 176), 0.0, Op.is_gt)
+        tt(W("Q2"), W("Q1"), W("DUMP"), Op.mult)
+        tt(W("WO"), W("Q2"), W("GL"), Op.max)
+        cp(W("WOU"), W("WO"))
+        op("V", lambda: g.vector.tensor_copy(T.TAB[:].indirect(T.WOU[:]), T.VAL[:]), [W("VAL"), W("WOU")], [W("TAB")])
+
+    prepare(0)
+    spread(1)
+    for t in range(VIS):
+        visit(t)
+        if t + 2 < VIS:
+            spread(t + 2)
+    cp(("TAB", 4095, 4096), ("XLAST", 15, 16))
+    dmas("S", "do4", [(T.ox[:], T.TAB[:, 0:4096], [W("TAB", 0, 4096)], [])])
+    for p, c in ev:
+        op("V", lambda p=p, c=c: g.vector.tensor_scalar(T.OG[:, p::2, :], T.GN[:, c:c + 128], -1.0, 4095.0, Op.mult, Op.add), [("GN", c, c + 128)], [("OG", c, c + 128)])
+    dmas("Y", "do1", [(T.og[:], T.OG[:], [W("OG")], [])])
+    new = W("AS", 256 * (VIS - 1), 256)
+    ts(W("AH"), new, 12, Op.arith_shift_right)
+    ts(W("BH"), new, 4095, Op.bitwise_and)
+    for p, c in ev:
+        op("V", lambda p=p, c=c: g.vector.tensor_scalar(T.OA[:, p::2, :], T.AH[:, c:c + 128], -1.0, 4095.0, Op.mult, Op.add), [("AH", c, c + 128)], [("OA", c, c + 128)])
+        op("V", lambda p=p, c=c: g.vector.tensor_scalar(T.OB[:, p::2, :], T.BH[:, c:c + 128], -1.0, 4095.0, Op.mult, Op.add), [("BH", c, c + 128)], [("OB", c, c + 128)])
+    dmas("Y", "do2", [(T.oa[:], T.OA[:], [W("OA")], [])])
+    dmas("Y", "do3", [(T.ob[:], T.OB[:], [W("OB")], [])])
+    for s in total:
+        take("G", (s, total[s]))

@@ -3,8 +3,18 @@ from concourse.mybir import dt, AluOpType as Op, ActivationFunctionType as Fn
 
 VIS = 5
 H = 65536.0
-F32, BF, I32, U16 = "float32", "bfloat16", "int32", "uint16"
+BIG = 8388608.0
+F32, F16, BF, I32, U16 = "float32", "float16", "bfloat16", "int32", "uint16"
 SCRATCH = {}
+WEIGHT = {"ID": 1.0, "NID": -1.0, "N16": -16.0, "NH": -H, "PH": H, "P4K": 4096.0, "P2K": 2048.0, "N2K": -2048.0, "P8M": BIG,
+          "HALF": 0.5, "N25": -0.25}
+MATF = {"I1F": 1.0}
+MATH = {"M101": -101.0, "M65": -65.0, "NIDH": -1.0, "PIDH": 1.0, "N4KH": -4096.0}
+MATS = list(WEIGHT) + ["MOD16", "BLK", "TRI", "ZER", "TMPC"]
+ALIAS = {}
+for _b, _l in (("MAT", MATS), ("MF", list(MATF)), ("MH", list(MATH))):
+    for _i, _n in enumerate(_l):
+        ALIAS[_n] = (_b, 128 * _i, 128 * _i + 128)
 
 
 def _declare(where, dtype, names):
@@ -14,31 +24,30 @@ def _declare(where, dtype, names):
 
 _declare("sbuf", BF, {
     "TAB": 4352, "XLAST": 16, "YV": 1280, "TH": 512, "XRM": 2048, "XRO": 2048, "XRN": 2048, "MX": 6144, "EQ": 2176,
-    "SEL2": 2048, "SELN": 2048, "DS": 2048, "WE": 1024, "TMPC": 128, "IDX": 16, "ID": 128, "NID": 128, "N16": 128,
-    "NH": 128, "PH": 128, "N4K": 128, "MOD16": 128, "BLK": 128, "TRI": 128, "ZER": 128, "ONES": 256, "FB": 256, "EB": 256,
-    "EA": 256, "HE2": 256, "OPB": 256, "TKO": 128, "MGB": 128, "FMB": 128, "NOM": 16, "OUTS": 256, "CS": 64,
-    "VR0": 2048, "VR1": 2048})
+    "SEL2": 2048, "SELN": 2048, "DS": 2048, "WE": 1024, "IDX": 16, "MAT": 128 * len(MATS), "ONES": 256, "FB": 256,
+    "EA": 256, "HE2": 256, "OPB": 256, "TKO": 128, "MGB": 128, "MTB": 128, "FMB": 128, "NOM": 16, "OUTS": 256, "CS": 256,
+    "SVX": (5, 128), "VAL": 256, "H1": 256, "H2": 256})
+_declare("sbuf", F16, {"CC": 256, "SELF": 128, "OPC": 256, "MH": 128 * len(MATH)})
 _declare("sbuf", I32, {
     "IOTA": 4096, "LG": (16, 16), "LA": (16, 16), "LBM": (16, 16), "LT": (16, 16), "THI": 512, "PM": 128, "PR": 128,
     "MC": 128, "TMPA": 128, "TMPB": 128, "C16": 16, "P15": 16, "PI": 256, "SH": 256, "S1": 256, "NHT": 256, "AH": 256,
-    "BH": 256, "VAL": 256, "AB_0": 256, "AS": 1280})
+    "BH": 256, "AB_0": 256, "AS": 1280, "SVI": 80, "SVH": (5, 16), "SVL": (5, 16)})
 _declare("sbuf", F32, {
-    "DUMP": 16, "N37F": 128, "N1F": 128, "GF": 256, "GH": 256, "SELF": 128, "TS": 256, "DXS": 256, "DGN": 256, "MN": 128,
-    "MNG": 128, "MNA": 128, "G0": 256, "DNN": 128, "GN": 256, "FN": 128, "TR": 112, "GL": 16, "H1": 256, "SUM": 256,
-    "Q1": 16, "Q2": 16, "WO": 16, "AB0": 256, "G4": 128, "DAB": 128, "OG": (16, 16), "OA": (16, 16), "OB": (16, 16)})
+    "DUMP": 16, "MF": 128 * len(MATF), "TS": 256, "DXS": 256, "DGN": 256, "MN": 128,
+    "MNG": 128, "MNA": 128, "G0": 256, "GN": 256, "FN": 128, "TR": 112, "GL": 16, "NMG": 128, "OPAF": 256, "OPBF": 256,
+    "TKN": 128, "VALF": 256, "A1": 128, "Q1": 16, "Q2": 16, "WO": 16, "OG": (16, 16), "OA": (16, 16), "OB": (16, 16)})
 _declare("sbuf", U16, {"SELU": 128, "NU": 128, "GLU": 16, "GR": 256, "OFU": 32, "WOU": 16, "GU0": 256, "GS": 1024})
-PSUM = ["PV", "PL", "PG", "PN", "PT", "PM1", "VB1", "VB2"]
+PSUM = ["PV", "PL", "PG", "PN", "PT", "PM1", "PX", "VB2"]
 _declare("psum", F32, {b: 512 for b in PSUM})
 for _t in range(1, VIS):
     _declare("sbuf", U16, {"GU%d" % _t: 256})
     _declare("sbuf", I32, {"AB_%d" % _t: 256})
-    _declare("sbuf", BF, {"CR%d" % _t: 16})
+    _declare("sbuf", BF, {"CR%d" % _t: 64})
 for _t in range(1, VIS - 1):
-    _declare("sbuf", BF, {"VT%d" % _t: 256, "TH%d" % _t: 512})
+    _declare("sbuf", BF, {"VT%d" % _t: 256, "TH%d" % _t: 512, "SV%d" % _t: 128})
 SEMAPHORES = (["qV", "qS", "qT", "qG", "lsem", "dx", "dxl", "dg", "da", "db", "dth", "dy", "do1", "do2", "do3", "do4"]
-              + ["vr%d" % t for t in range(VIS)]
               + [n + "%d" % t for t in range(1, VIS) for n in ("ag", "ab", "ac")]
-              + [n + "%d" % t for t in range(1, VIS - 1) for n in ("av", "at")])
+              + [n + "%d" % t for t in range(1, VIS - 1) for n in ("av", "at", "as")])
 
 
 def rank_program(g, core, T, topo):
@@ -107,8 +116,15 @@ def rank_program(g, core, T, topo):
         for (o, i, reads, writes) in items:
             note("dma" + sem, reads, writes, tok)
 
+    def W(b, a=0, n=None):
+        if b in ALIAS:
+            return ALIAS[b]
+        return (b, a, a + (n if n is not None else int(np.prod(SCRATCH[b][1][1:])) - a))
+
     def R(r):
         b, a, e = r
+        if b == "SVX":
+            return T.SVX[:, a // 128, a % 128:a % 128 + e - a]
         return T[b][:, a:e]
 
     def tt(o, a, b, f):
@@ -143,8 +159,6 @@ def rank_program(g, core, T, topo):
             return last
         op("T", call, list(dict.fromkeys(reads)), [o_all])
 
-    def W(b, a=0, n=None):
-        return (b, a, a + (n if n is not None else int(np.prod(SCRATCH[b][1][1:])) - a))
     mat = lambda b, s=0: (b, 128 * s, 128 * s + 128)
     nxt = {0: [(0, 128, 128)], 128: [(0, 16, 112), (112, 0, 16)]}
     prv = {128: [(0, 0, 128)], 0: [(0, 240, 16), (16, 128, 112)]}
@@ -169,18 +183,13 @@ def rank_program(g, core, T, topo):
     dmas("Y", "db", [(T.LBM[:], T.bl[:], [], [W("LBM")])])
     dmas("Y", "dxl", [(T.XLAST[:], T.xt[:, 4080:4096], [], [W("XLAST")])])
     for t in range(1, VIS - 1):
-        arrives((rank - t) % 4, W("VT%d" % t), "av%d" % t)
-        arrives((rank - t) % 4, W("TH%d" % t), "at%d" % t)
+        for b, sem in (("VT", "av"), ("TH", "at"), ("SV", "as")):
+            arrives((rank - t) % 4, W("%s%d" % (b, t)), "%s%d" % (sem, t))
     for t in range(1, VIS):
-        arrives((rank - 1) % 4, W("GU%d" % t), "ag%d" % t)
-        arrives((rank - 1) % 4, W("AB_%d" % t), "ab%d" % t)
-        arrives((rank - 1) % 4, W("CR%d" % t), "ac%d" % t)
-    view = lambda t: W("YV", 256 * t, 256) if t in (0, VIS - 1) else W("VT%d" % t)
-    thr = lambda t: "TH" if t in (0, VIS - 1) else "TH%d" % t
-
-    def spread(t):
-        v, d = view(t), "VR%d" % (t % 2)
-        dmas("Y", "vr%d" % t, [(T[d][:, 256 * k:256 * k + 256], R(v), [v], [(d, 256 * k, 256 * k + 256)]) for k in range(8)])
+        for b, sem in (("GU%d", "ag"), ("AB_%d", "ab"), ("CR%d", "ac")):
+            arrives((rank - 1) % 4, W(b % t), "%s%d" % (sem, t))
+    home = lambda t: t in (0, VIS - 1)
+    view = lambda t: W("YV", 256 * t, 256) if home(t) else W("VT%d" % t)
 
     def iota(b, pat, base, cm):
         op("G", lambda: g.iota(T[b][:], pat, base, cm), [], [W(b)])
@@ -188,34 +197,46 @@ def rank_program(g, core, T, topo):
     iota("PR", [[0, 128]], 0, 1)
     iota("MC", [[1, 128]], 0, 0)
     iota("C16", [[16, 16]], 0, 0)
-    for b, c in (("SELN", 0.0), ("SEL2", 0.0), ("ONES", 1.0), ("ZER", 0.0)):
-        op("V", lambda b=b, c=c: g.vector.memset(T[b][:], c), [], [W(b)])
-    ts(W("N37F"), W("PM"), 128.0, Op.is_equal, -37.0, Op.mult)
-    ts(W("N1F"), W("PM"), 128.0, Op.is_equal, -1.0, Op.mult)
-    for b, c in (("ID", 1.0), ("NID", -1.0), ("N4K", -4096.0), ("NH", -H), ("PH", H), ("N16", -16.0)):
-        ts(W(b), W("PM"), 128.0, Op.is_equal, c, Op.mult)
+    for b, c in ((W("SELN"), 0.0), (W("ONES"), 1.0), (W("ZER"), 0.0)):
+        op("V", lambda b=b, c=c: g.vector.memset(R(b), c), [], [b])
+    act(W("SEL2"), W("SELN"), 0.0)
+    act(W("DS"), W("SELN"), 0.0)
     ts(W("TMPA"), W("PR"), 4, Op.arith_shift_right)
     ts(W("TMPB"), W("MC"), 4, Op.arith_shift_right)
     tt(W("BLK"), W("TMPA"), W("TMPB"), Op.is_equal)
+    blk = ALIAS["BLK"][1]
+    for d in (MATH, WEIGHT, MATF):
+        for b, c in d.items():
+            ts(W(b), W("PM"), 128.0, Op.is_equal, c, Op.mult)
     for s in range(16):
         z = (slice(None), slice(128 * s + s, 128 * s + 128, 16))
-        f = (slice(None), slice(s, 128, 16))
-        op("V", lambda z=z, f=f: g.vector.tensor_scalar(T.SELN[z], T.BLK[f], -1.0, None, Op.mult), [W("BLK")], [mat("SELN", s)])
-        op("S", lambda z=z, f=f: g.scalar.activation(T.SEL2[z], T.BLK[f], Fn.Identity, bias=0.0, scale=2.0), [W("BLK")], [mat("SEL2", s)])
+        f = (slice(None), slice(blk + s, blk + 128, 16))
+        op("V", lambda z=z, f=f: g.vector.tensor_scalar(T.SELN[z], T.MAT[f], -1.0, None, Op.mult), [W("BLK")], [mat("SELN", s)])
+        op("S", lambda z=z, f=f: g.scalar.activation(T.SEL2[z], T.MAT[f], Fn.Identity, bias=0.0, scale=2.0), [W("BLK")], [mat("SEL2", s)])
+    for s in range(16):
+        op("S", lambda s=s: g.scalar.activation(T.DS[:, 128 * s + s:128 * s + 128:16], T.MAT[:, s:128:16], Fn.Copy), [W("ID")], [mat("DS", s)])
+    act(("TAB", 4095, 4096), ("ONES", 0, 1), 1024.0)
 
     ev = [(0, 0), (1, 128)]
     for p, c in ev:
         op("V", lambda p=p, c=c: g.vector.tensor_copy(T.GU0[:, c:c + 128], T.LG[:, p::2, :]), [W("LG")], [("GU0", c, c + 128)])
+    for t in range(1, VIS - 1):
+        send((rank + t) % 4, W("VT%d" % t), W("YV", 256 * t, 256), "av%d" % t)
+    iota("IOTA", [[1, 4096]], 0, 0)
+    for p, c in ev:
         op("V", lambda p=p, c=c: g.vector.tensor_scalar(T.THI[:, c:c + 128], T.LT[:, p::2, :], 15, None, Op.bitwise_and), [W("LT")], [("THI", c, c + 128)])
         op("V", lambda p=p, c=c: g.vector.tensor_scalar(T.THI[:, 256 + c:384 + c], T.LT[:, p::2, :], 4, None, Op.arith_shift_right), [W("LT")], [("THI", 256 + c, 384 + c)])
     cp(W("TH"), W("THI"))
-    for t in range(1, VIS - 1):
-        send((rank + t) % 4, W("VT%d" % t), W("YV", 256 * t, 256), "av%d" % t)
+    mms(("PN", 0, 80), [(("PN", 0, 80), mat("SELN", s), (W("YV"), s)) for s in range(16)], True, True)
+    ts(W("SVI"), ("PN", 0, 80), -1.0, Op.mult)
+    op("V", lambda: g.vector.tensor_scalar(T.SVH[:], T.SVI[:], 4, None, Op.arith_shift_right), [W("SVI")], [W("SVH")])
+    op("V", lambda: g.vector.tensor_scalar(T.SVL[:], T.SVI[:], 15, None, Op.bitwise_and), [W("SVI")], [W("SVL")])
+    for r in range(4):
+        for b, c in (("SVH", 16 * r), ("SVL", 64 + 16 * r)):
+            op("V", lambda b=b, c=c: g.vector.tensor_copy(T.SVX[:, :, c:c + 16], T[b][:]), [W(b)], [W("SVX")])
     for t in range(1, VIS - 1):
         send((rank + t) % 4, W("TH%d" % t), W("TH"), "at%d" % t)
-    spread(0)
-    op("V", lambda: g.vector.memset(T.TAB[:, 4095:4096], 1024.0), [], [("TAB", 4095, 4096)])
-    iota("IOTA", [[1, 4096]], 0, 0)
+        send((rank + t) % 4, W("SV%d" % t), W("SVX", 128 * t, 128), "as%d" % t)
 
     def late():
         for p, c in ev:
@@ -233,17 +254,10 @@ def rank_program(g, core, T, topo):
         ts(W("P15"), ("PR", 0, 16), 15, Op.bitwise_and)
         tt(W("IDX"), W("C16"), W("P15"), Op.add)
         ts(W("DUMP"), W("IDX"), 4096.0, Op.add)
-        op("V", lambda: g.vector.memset(T.DS[:], 0.0), [], [W("DS")])
-        for s in range(16):
-            op("V", lambda s=s: g.vector.tensor_copy(T.DS[:, 128 * s + s:128 * s + 128:16], T.ID[:, s:128:16]), [W("ID")], [mat("DS", s)])
 
     def prepare(t):
-        v = view(t)
-        mms(W("PV"), [(("PV", 0, 256), W("ID"), v)], True, True)
-        mms(W("PV"), [(("PV", 256, 512), W("ID"), v)], True, True)
-        th, vr = thr(t), "VR%d" % (t % 2)
-        mms(("PT", 0, 256), [(("PT", 0, 256), W("NID"), (th, 0, 256)), (("PT", 0, 256), W("N16"), (th, 256, 512))], True, False)
-        mms(("PT", 0, 256), [(("PT", h, h + 128), mat("SELN", s), (W(vr), s)) for h in (0, 128) for s in range(16)], False, False)
+        for h in (0, 256):
+            mms(W("PV"), [(("PV", h, h + 256), W("ID"), view(t))], True, True)
 
     def visit(t):
         M = 0 if t % 2 == 0 else 128
@@ -251,7 +265,9 @@ def rank_program(g, core, T, topo):
         hm = lambda b: (b, M, M + 128)
         ho = lambda b: (b, O, O + 128)
         gu = W("GU%d" % t)
+        ab = W("AB_%d" % t)
         last = t == VIS - 1
+        ones = ("ONES", 0, 128)
 
         def gather(out, c, lst, lc):
             op("S", lambda: g.scalar.activation(T[out][:, 1024 * c:1024 * c + 1024], T.TAB[:, 0:4096].indirect(T[lst][:, lc:lc + 64]), Fn.Copy),
@@ -262,111 +278,154 @@ def rank_program(g, core, T, topo):
                 a, z = 1024 * c + 512 * h, 1024 * n + 512 * h
                 tt(("MX", z, z + 512), (x, a, a + 512), W("PV"), Op.max)
 
-        def sums(x, c, n, bank, col, extra=()):
+        def sumx(x, c, bank, col, extra=()):
             out = (bank, col, col + 64)
             mms(out, [(out, mat("SELN", s), ((x, 1024 * c, 1024 * c + 1024), s)) for s in range(16)] + [(out, l, r) for l, r in extra], True, False)
+
+        def sum2(n, bank, col):
+            out = (bank, col, col + 64)
             mms(out, [(out, mat("SEL2", s), (("MX", 1024 * n, 1024 * n + 1024), s)) for s in range(16)], False, True)
 
         gather("XRM", 0, gu[0], M)
         gather("XRM", 1, gu[0], M + 64)
-        cp(W("GF"), gu)
-        mms(("PL", 0, 256), [(("PL", 0, 256), W("NID"), W("ONES")), (("PL", 0, 256), W("N37F"), W("GF"))]
-            + [(("PL", b + d, b + d + n), W("N1F"), ("GF", s, s + n)) for b in (0, 128) for d, s, n in nxt[b]], True, True)
+        ts(W("CC"), gu, -2048.0, Op.add)
+        r = ("PL", 0, 256)
+        mms(r, [(r, W("NID"), W("ONES")), (r, W("M101"), W("CC"))]
+            + [(("PL", b + d, b + d + n), W("M65"), ("CC", s, s + n)) for b in (0, 128) for d, s, n in nxt[b]], True, True)
         ts(W("FB"), gu, 4095.0, Op.is_lt)
-        mms(("PL", 256, 384), [(("PL", 256, 384), W("N4K"), ho("FB"))], True, True)
+        r = ("PL", 256, 384)
+        mms(r, [(r, W("P4K"), ho("FB")), (r, W("P2K"), ones), (r, W("NID"), ones)], True, True)
         for b in (0, 128):
             for d, s, n in nxt[b]:
-                tt(("PI", b + d, b + d + n), ("GF", b + d, b + d + n), ("GF", s, s + n), Op.mult)
+                tt(("PI", b + d, b + d + n), ("CC", b + d, b + d + n), ("CC", s, s + n), Op.mult)
         ts(W("SH"), W("PI"), 5, Op.arith_shift_right)
-        ts(W("GH"), gu, -1.0, Op.mult, 4095.0, Op.add)
         tt(W("S1"), ("PL", 0, 256), W("SH"), Op.subtract)
         ts(W("NHT"), W("S1"), 4095, Op.bitwise_and)
-        tt(("VB1", 0, 128), ("PL", 256, 384), ho("NHT"), Op.add)
-        tt(W("SELF"), ("VB1", 0, 128), ho("GH"), Op.max)
-        ts(W("SELU"), W("SELF"), -1.0, Op.mult, 4095.0, Op.add)
+        tt(("VB2", 0, 128), ("PL", 256, 384), ho("NHT"), Op.subtract)
         ts(W("NU"), hm("NHT"), -1.0, Op.mult, 4095.0, Op.add)
-        ts(W("EB"), gu, 4095.0, Op.is_ge)
-        ts(hm("HE2"), hm("EB"), 2 * H, Op.mult, H, Op.add)
+        tt(W("SELF"), ("VB2", 0, 128), ho("CC"), Op.min)
+        ts(hm("HE2"), hm("FB"), -2 * H, Op.mult, 2 * H, Op.add)
+        ts(W("SELU"), W("SELF"), 2048.0, Op.add)
+        th, sv, z = ("TH", "SVX", 128 * t) if home(t) else ("TH%d" % t, "SV%d" % t, 0)
+        r = ("PT", 0, 256)
+        mms(r, [(r, W("NID"), (th, 0, 256)), (r, W("N16"), (th, 256, 512))]
+            + [(("PT", h, h + 64), W(m), (sv, z + c, z + c + 64)) for h in range(0, 256, 64) for m, c in (("N16", 0), ("NID", 64))], True, False)
+        px = ("PX", 0, 256)
+        mms(px, [(px, W("P2K"), W("ONES")), (px, W("NID"), W("ONES")), (px, W("NIDH"), W("CC"))], True, False)
         if t == 0:
             later()
         gather("XRO", 0, "SELU", 0)
         gather("XRO", 1, "SELU", 64)
         maxes("XRM", 0, 0)
-        sums("XRM", 0, 0, "PG", M)
+        sumx("XRM", 0, "PG", M)
+        sum2(0, "PG", M)
         maxes("XRM", 1, 1)
-        sums("XRM", 1, 1, "PG", M + 64)
+        sumx("XRM", 1, "PG", M + 64)
+        sum2(1, "PG", M + 64)
         if t == 0:
             late()
-        if t > 0:
-            mms(("PT", 0, 256), [(("PT", 16 * k, 16 * k + 16), W("NID"), W("CR%d" % t)) for k in range(16)], False, False)
-        ab = W("AB_%d" % t)
         gather("XRN", 0, "NU", 0)
         maxes("XRO", 0, 2)
-        sums("XRO", 0, 2, "PG", O, [(W("NH"), ("EB", O, O + 64))])
+        sumx("XRO", 0, "PG", O, [(W("PH"), ("FB", O, O + 64))])
+        sum2(2, "PG", O)
         ts(W("EA"), ab, 4096.0, Op.is_lt)
-        mms(("PT", 0, 256), [(("PT", 0, 256), W("NH"), W("EB"))]
-            + [(("PT", b + d, b + d + n), W("PH"), ("EB", s, s + n)) for b in (0, 128) for d, s, n in nxt[b]]
-            + [(("PT", 0, 256), W("NH"), W("EA"))], False, True)
+        r = ("PT", 0, 256)
+        mms(r, ([(("PT", h, h + 64), W("NID"), W("CR%d" % t)) for h in range(0, 256, 64)] if t > 0 else [])
+            + [(r, W("PH"), W("FB")), (("PT", O, O + 128), W("NH"), ones)]
+            + [(("PT", b + d, b + d + n), W("NH"), ("FB", s, s + n)) for b in (0, 128) for d, s, n in nxt[b]]
+            + [(r, W("NH"), W("EA"))], False, True)
         ts(W("AH"), ab, 12, Op.arith_shift_right)
         ts(W("BH"), ab, 4095, Op.bitwise_and)
         maxes("XRO", 1, 3)
-        sums("XRO", 1, 3, "PG", O + 64, [(W("NH"), ("EB", O + 64, O + 128))])
+        sumx("XRO", 1, "PG", O + 64, [(W("PH"), ("FB", O + 64, O + 128))])
+        sum2(3, "PG", O + 64)
         act(W("TS"), ("PT", 0, 256), -1.0, H)
-        act(ho("DXS"), ho("PG"))
+        act(ho("DXS"), ho("PG"), 1.0, -H)
         gather("XRN", 1, "NU", 64)
-        act(W("G4"), hm("GH"), 4096.0)
         maxes("XRN", 0, 4)
-        sums("XRN", 0, 4, "PN", 0)
+        sumx("XRN", 0, "PN", 0)
+        sum2(4, "PN", 0)
         tt(W("OPB"), ("PG", 0, 256), W("TS"), Op.is_gt)
-        mms(("PL", 0, 128), [(("PL", 0, 128), W("NH"), hm("EB"))] + [(("PL", d, d + n), W("NH"), ("OPB", s, s + n)) for d, s, n in nxt[M]], True, True)
-        mms(("PL", 128, 256), [(("PL", 128, 256), W("NH"), hm("FB"))] + [(("PL", 128 + d, 128 + d + n), W("NH"), ("OPB", s, s + n)) for d, s, n in prv[M]], True, True)
+        r = ("PM1", 256, 512)
+        mms(r, [(r, W("ID"), W("OPB"))], True, True)
+        mms(px, [(px, W("N2K"), W("OPB")), (px, W("ID"), W("OPB"))], False, False)
+        r = ("PL", 0, 128)
+        mms(r, [(r, W("PH"), hm("FB")), (r, W("NH"), ones)] + [(("PL", d, d + n), W("NH"), ("OPB", s, s + n)) for d, s, n in nxt[M]], True, True)
+        r = ("PL", 128, 256)
+        mms(r, [(r, W("NH"), hm("FB"))] + [(("PL", 128 + d, 128 + d + n), W("NH"), ("OPB", s, s + n)) for d, s, n in prv[M]], True, True)
         tt(hm("DGN"), hm("PG"), hm("HE2"), Op.subtract)
-        for d, s, n in nxt[O]:
-            tt(("VB2", d, d + n), ("PG", O + d, O + d + n), ("DGN", s, s + n), Op.is_lt)
-        for d, s, n in prv[O]:
-            tt(("TKO", d, d + n), ("VB2", d, d + n), ("OPB", s, s + n), Op.is_gt)
-        mms(("PL", 256, 512), [(("PL", 256, 512), W("ID"), W("ONES")), (("PL", 256, 512), W("NID"), W("OPB"))]
-            + [(("PL", 256 + b + d, 256 + b + d + n), W("NID"), ("OPB", s, s + n)) for b in (0, 128) for d, s, n in prv[b]]
-            + [(("PL", 256 + O, 384 + O), W("NID"), W("TKO"))], True, True)
-        tt(("VB1", 0, 256), ("PG", 0, 256), W("TS"), Op.is_gt)
         for d, s, n in nxt[M]:
             tt(("MN", d, d + n), ("PG", M + d, M + d + n), ("DXS", s, s + n), Op.min)
-        maxes("XRN", 1, 5)
-        sums("XRN", 1, 5, "PN", 64)
-        tt(("VB1", 256, 512), ("VB1", 0, 256), W("AH"), Op.mult)
-        tt(("VB1", 0, 256), ("VB1", 0, 256), W("BH"), Op.mult)
+        for d, s, n in nxt[O]:
+            tt(("VB2", d, d + n), ("PG", O + d, O + d + n), ("DGN", s, s + n), Op.is_lt)
+        tt(W("OPAF"), ("PM1", 256, 512), W("AH"), Op.mult)
+        mms(px, [(px, W("I1F"), W("OPAF"))], False, False)
+        tt(W("OPBF"), ("PM1", 256, 512), W("BH"), Op.mult)
+        mms(px, [(("PX", b + d, b + d + n), W("I1F"), ("OPBF", s, s + n)) for b in (0, 128) for d, s, n in prv[b]], False, False)
+        for d, s, n in prv[O]:
+            tt(("TKO", d, d + n), ("VB2", d, d + n), ("OPB", s, s + n), Op.is_gt)
+        tt(W("OPC"), ("PM1", 256, 512), W("CC"), Op.mult)
+        tt(W("TKN"), W("TKO"), ho("NHT"), Op.mult)
+        sumx("XRN", 1, "PN", 64)
+        mms(px, [(px, W("PIDH"), W("OPC"))], False, False)
+        mms(px, [(("PX", O, O + 128), W("I1F"), W("TKN"))], False, True)
         tt(W("MNG"), ("PL", 0, 128), W("MN"), Op.add)
         tt(("VB2", 128, 256), ("PL", 128, 256), W("MN"), Op.add)
+        maxes("XRN", 1, 5)
+        sum2(5, "PN", 64)
         tt(W("MNA"), ("VB2", 128, 256), W("MNG"), Op.max)
-        tt(W("G0"), ("PL", 256, 512), W("GH"), Op.mult)
-        tt(W("G0"), ("VB1", 256, 512), W("G0"), Op.add)
-        for b in (0, 128):
-            for d, s, n in prv[b]:
-                tt(("G0", b + d, b + d + n), ("VB1", s, s + n), ("G0", b + d, b + d + n), Op.add)
-        tt(("VB2", 0, 128), W("TKO"), ho("NHT"), Op.mult)
-        tt(ho("G0"), ("VB2", 0, 128), ho("G0"), Op.add)
-        tt(W("DNN"), hm("NHT"), hm("G0"), Op.subtract)
+        gx = ("PX", M, M + 128)
+        tt(("VB2", 256, 384), gx, hm("NHT"), Op.subtract)
         tt(W("MGB"), ("PN", 0, 128), W("MNG"), Op.is_lt)
-        tt(("VB2", 256, 384), ("PN", 0, 128), W("MNA"), Op.is_lt)
-        tt(("VB2", 384, 512), ("PN", 0, 128), W("MNG"), Op.is_ge)
-        mms(("PM1", 0, 128), [(("PM1", 0, 128), W("N16"), W("MGB"))]
-            + [(("PM1", 16 * d, 128), W("ID"), ("MGB", 0, 128 - 16 * d)) for d in range(1, 8)], True, True)
+        r = ("PM1", 0, 128)
+        mms(r, [(r, W("N16"), W("MGB"))] + [(("PM1", 16 * d, 128), W("ID"), ("MGB", 0, 128 - 16 * d)) for d in range(1, 8)], True, True)
+        tt(W("MTB"), ("PN", 0, 128), W("MNA"), Op.is_lt)
+        tt(W("NMG"), ("PN", 0, 128), W("MNG"), Op.is_ge)
         if not last:
-            mms(("PT", 0, 16), [(("PT", 0, 16), W("MOD16"), ("MGB", 16 * e, 16 * e + 16)) for e in range(8)], True, True)
-            act(W("CS", 16 * t, 16), ("PT", 0, 16))
-        tt(("VB1", 0, 128), ("VB2", 256, 384), W("DNN"), Op.mult)
-        tt(hm("GN"), ("VB1", 0, 128), hm("G0"), Op.add)
-        for d, s, n in prv[O]:
-            tt(("GN", O + d, O + d + n), ("VB2", 384 + s - M, 384 + s - M + n), ("G0", O + d, O + d + n), Op.mult)
+            r = ("PT", 0, 16)
+            mms(r, [(r, W("MOD16"), ("MGB", 16 * e, 16 * e + 16)) for e in range(8)], True, True)
+            for k in range(4):
+                act(W("CS", 64 * t + 16 * k, 16), r)
+
+        def places():
+            tt(hm("G0"), ("VB2", 256, 384), W("MTB"), Op.mult)
+            for d, s, n in prv[O]:
+                tt(("GN", O + d, O + d + n), ("PX", O + d, O + d + n), ("NMG", s - M, s - M + n), Op.mult)
+            tt(hm("GN"), gx, hm("G0"), Op.subtract)
+
+        def memories():
+            z = 256 * t
+            tt(("AS", z + O, z + O + 128), ("PL", 256 + O, 384 + O), ho(ab[0]), Op.mult)
+            tt(("VB2", 384, 512), ("PL", 256 + M, 384 + M), hm(ab[0]), Op.mult)
+            tt(W("A1"), ("PX", 256, 384), W("MGB"), Op.mult)
+            tt(("AS", z + M, z + M + 128), ("VB2", 384, 512), W("A1"), Op.add)
+            if not last:
+                send((rank + 1) % 4, W("AB_%d" % (t + 1)), W("AS", z, 256), "ab%d" % (t + 1))
+
         if not last:
+            places()
             ts(W("GS", 256 * t, 256), W("GN"), -1.0, Op.mult, 4095.0, Op.add)
             send((rank + 1) % 4, W("GU%d" % (t + 1)), W("GS", 256 * t, 256), "ag%d" % (t + 1))
-            send((rank + 1) % 4, W("CR%d" % (t + 1)), W("CS", 16 * t, 16), "ac%d" % (t + 1))
+            send((rank + 1) % 4, W("CR%d" % (t + 1)), W("CS", 64 * t, 64), "ac%d" % (t + 1))
+        kp = ("PL", 256, 512)
+        mms(kp, [(kp, W("ID"), W("ONES")), (kp, W("NID"), W("OPB"))]
+            + [(("PL", 256 + b + d, 256 + b + d + n), W("NID"), ("OPB", s, s + n)) for b in (0, 128) for d, s, n in prv[b]]
+            + [(("PL", 256 + O, 384 + O), W("NID"), W("TKO")), (("PL", 256 + M, 384 + M), W("NID"), W("MTB"))]
+            + [(("PL", 256 + O + d, 256 + O + d + n), W("NID"), ("MGB", s - M, s - M + n)) for d, s, n in prv[O]], True, True)
         ts(W("FMB"), ("PM1", 0, 128), -16.0, Op.is_equal)
         sh = t % 2
         for k in range(1 + sh):
-            o = ("PM1", 128 + 16 * k, 144 + 16 * k)
-            mms(o, [(o, W("ID"), W("IDX"))] + [(o, mat("WE", (e + k) % 8), ("FMB", 16 * e, 16 * e + 16)) for e in range(8)], True, True)
+            r = ("PM1", 128 + 16 * k, 144 + 16 * k)
+            mms(r, [(r, W("ID"), W("IDX"))] + [(r, mat("WE", (e + k) % 8), ("FMB", 16 * e, 16 * e + 16)) for e in range(8)], True, True)
+        pt = ("PT", 256, 512)
+        mms(pt, [(pt, W("ZER"), W("ONES"))], True, False)
+
+        def both():
+            r = ("PX", 256, 384)
+            mms(r, [(r, W("P8M"), ones), (r, W("N2K"), ones), (r, W("NID"), ones), (r, W("N4KH"), hm("CC"))]
+                + [(("PX", 256 + d, 256 + d + n), W("NIDH"), ("CC", s, s + n)) for d, s, n in nxt[M]], True, True)
+        if not last:
+            both()
         tt(W("FN"), W("FMB"), hm("NHT"), Op.mult)
         tt(("TR", 0, 64), ("FN", 0, 64), ("FN", 64, 128), Op.add)
         tt(("TR", 64, 96), ("TR", 0, 32), ("TR", 32, 64), Op.add)
@@ -375,8 +434,8 @@ def rank_program(g, core, T, topo):
         ts(W("GL"), ("TR", 96, 112), -1.0, Op.mult, 4095.0, Op.add)
         op("V", lambda: g.vector.tensor_copy(T.GR[:], T.IOTA[:].indirect(T.GLU[:])), [W("IOTA"), W("GLU")], [W("GR")])
         cp(("OFU", 0, 16 + 16 * sh), ("PM1", 128, 144 + 16 * sh))
-        op("S", lambda: g.scalar.activation(T.H1[:], T.XRM[:].indirect(T.OFU[:, 0:16]), Fn.Copy), [W("XRM"), ("OFU", 0, 16)], [W("H1")])
-        mms(("PT", 256, 512), [(("PT", 256, 512), W("ZER"), W("ONES"))], True, False)
+        for h, x, c in (("H1", "XRM", 0), ("H2", "XRO", 16 * sh)):
+            op("S", lambda h=h, x=x, c=c: g.scalar.activation(T[h][:], T[x][:].indirect(T.OFU[:, c:c + 16]), Fn.Copy), [W(x), ("OFU", c, c + 16)], [W(h)])
         at = 0
         for c in range(16):
             n = 256 - 16 * c
@@ -385,53 +444,45 @@ def rank_program(g, core, T, topo):
             it = [(("PT", 256 + 16 * c, 272 + 16 * c), W("TRI"), ("EQ", at, at + 16))]
             if n > 16:
                 it.append((("PT", 272 + 16 * c, 512), W("BLK"), ("EQ", at + 16, at + n)))
-            mms(("PT", 256, 512), it, False, c == 15)
+            mms(pt, it, False, c == 15)
             at += n
-        act(W("OUTS"), ("PT", 256, 512))
         ts(W("NOM"), ("TR", 96, 112), 0.0, Op.is_equal)
-        mms(("PM1", 160, 176), [(("PM1", 160, 176), W("ID"), W("NOM"))]
-            + [(("PM1", 160, 176), mat("DS", s), (W("OUTS"), s)) for s in range(16)], True, True)
+        cp(W("OUTS"), pt)
+        nm = ("PN", 256, 512)
+        mms(nm, [(nm, W("HALF"), W("H1")), (nm, W("HALF"), W("H2")), (nm, W("N25"), W("ONES"))], True, True)
+        r = ("PM1", 160, 176)
+        mms(r, [(r, W("ID"), W("NOM"))] + [(r, mat("DS", s), (W("OUTS"), s)) for s in range(16)], True, True)
+        act(W("VALF"), nm, 1.0, BIG)
+        act(W("VAL"), W("VALF"), 1.0, -BIG)
         if not last:
             prepare(t + 1)
-        op("V", lambda: g.vector.tensor_tensor(T.SUM[:], T.XRO[:].indirect(T.OFU[:, 16 * sh:16 * sh + 16]), T.H1[:], Op.add),
-           [W("XRO"), W("H1"), ("OFU", 16 * sh, 16 * sh + 16)], [W("SUM")])
-        ts(W("VAL"), W("SUM"), 0.5, Op.mult, -0.25, Op.add)
-        z = 256 * t
-        tt(W("AB0"), ("PL", 256, 512), ab, Op.mult)
-        for d, s, n in nxt[M]:
-            tt(("VB1", d, d + n), ("GH", s, s + n), ("FB", M + d, M + d + n), Op.mult)
-        tt(("VB1", 128, 256), ("VB1", 0, 128), W("G4"), Op.add)
-        tt(W("DAB"), ("VB1", 128, 256), hm("AB0"), Op.subtract)
-        tt(("VB1", 256, 384), ("VB2", 256, 384), W("DAB"), Op.mult)
-        tt(("AS", z + M, z + M + 128), ("VB1", 256, 384), hm("AB0"), Op.add)
-        for d, s, n in prv[O]:
-            tt(("AS", z + O + d, z + O + d + n), ("VB2", 384 + s - M, 384 + s - M + n), ("AB0", O + d, O + d + n), Op.mult)
-        if not last:
-            send((rank + 1) % 4, W("AB_%d" % (t + 1)), W("AS", z, 256), "ab%d" % (t + 1))
-        ts(W("Q1"), ("PM1", 160, 176), 0.0, Op.is_gt)
+            memories()
+        ts(W("Q1"), r, 0.0, Op.is_gt)
         tt(W("Q2"), W("Q1"), W("DUMP"), Op.mult)
         tt(W("WO"), W("Q2"), W("GL"), Op.max)
         cp(W("WOU"), W("WO"))
         op("V", lambda: g.vector.tensor_copy(T.TAB[:].indirect(T.WOU[:]), T.VAL[:]), [W("VAL"), W("WOU")], [W("TAB")])
+        if last:
+            cp(("TAB", 4095, 4096), ("XLAST", 15, 16))
+            dmas("S", "do4", [(T.ox[:], T.TAB[:, 0:4096], [W("TAB", 0, 4096)], [])])
+            places()
+            both()
+            memories()
 
     prepare(0)
-    spread(1)
     for t in range(VIS):
         visit(t)
-        if t + 2 < VIS:
-            spread(t + 2)
-    cp(("TAB", 4095, 4096), ("XLAST", 15, 16))
-    dmas("S", "do4", [(T.ox[:], T.TAB[:, 0:4096], [W("TAB", 0, 4096)], [])])
-    for p, c in ev:
-        op("V", lambda p=p, c=c: g.vector.tensor_scalar(T.OG[:, p::2, :], T.GN[:, c:c + 128], -1.0, 4095.0, Op.mult, Op.add), [("GN", c, c + 128)], [("OG", c, c + 128)])
-    dmas("Y", "do1", [(T.og[:], T.OG[:], [W("OG")], [])])
+
+    def put(dst, src, sem, out):
+        for p, c in ev:
+            op("V", lambda p=p, c=c: g.vector.tensor_scalar(T[dst][:, p::2, :], T[src][:, c:c + 128], -1.0, 4095.0, Op.mult, Op.add),
+               [(src, c, c + 128)], [(dst, c, c + 128)])
+        dmas("Y", sem, [(T[out][:], T[dst][:], [W(dst)], [])])
+    put("OG", "GN", "do1", "og")
     new = W("AS", 256 * (VIS - 1), 256)
     ts(W("AH"), new, 12, Op.arith_shift_right)
+    put("OA", "AH", "do2", "oa")
     ts(W("BH"), new, 4095, Op.bitwise_and)
-    for p, c in ev:
-        op("V", lambda p=p, c=c: g.vector.tensor_scalar(T.OA[:, p::2, :], T.AH[:, c:c + 128], -1.0, 4095.0, Op.mult, Op.add), [("AH", c, c + 128)], [("OA", c, c + 128)])
-        op("V", lambda p=p, c=c: g.vector.tensor_scalar(T.OB[:, p::2, :], T.BH[:, c:c + 128], -1.0, 4095.0, Op.mult, Op.add), [("BH", c, c + 128)], [("OB", c, c + 128)])
-    dmas("Y", "do2", [(T.oa[:], T.OA[:], [W("OA")], [])])
-    dmas("Y", "do3", [(T.ob[:], T.OB[:], [W("OB")], [])])
+    put("OB", "BH", "do3", "ob")
     for s in total:
         take("G", (s, total[s]))

import numpy as np
from concourse.mybir import dt, AluOpType as Op, ActivationFunctionType as Fn

VIS = 5
H = 65536.0
BIG = 8388608.0
F32, F16, BF, I32, U16 = "float32", "float16", "bfloat16", "int32", "uint16"
SCRATCH = {}
WEIGHT = {"ID": 1.0, "NID": -1.0, "N16": -16.0, "NH": -H, "PH": H, "P4K": 4096.0, "P2K": 2048.0, "N2K": -2048.0, "P8M": BIG,
          "HALF": 0.5, "N25": -0.25}
MATF = {"I1F": 1.0}
MATH = {"M101": -101.0, "M65": -65.0, "NIDH": -1.0, "PIDH": 1.0, "N4KH": -4096.0}
MATS = list(WEIGHT) + ["MOD16", "BLK", "TRI", "ZER", "TMPC"]
ALIAS = {}
for _b, _l in (("MAT", MATS), ("MF", list(MATF)), ("MH", list(MATH))):
    for _i, _n in enumerate(_l):
        ALIAS[_n] = (_b, 128 * _i, 128 * _i + 128)


def _declare(where, dtype, names):
    for name, shape in names.items():
        SCRATCH[name] = (where, [128] + (list(shape) if isinstance(shape, tuple) else [shape]), dtype)


_declare("sbuf", BF, {
    "TAB": 4352, "XLAST": 16, "YV": 1280, "TH": 512, "XRM": 2048, "XRO": 2048, "XRN": 2048, "MX": 6144, "EQ": 2176,
    "SEL2": 2048, "SELN": 2048, "DS": 2048, "WE": 1024, "IDX": 16, "MAT": 128 * len(MATS), "ONES": 256, "FB": 256,
    "EA": 256, "HE2": 256, "OPB": 256, "TKO": 128, "MGB": 128, "MTB": 128, "FMB": 128, "NOM": 16, "OUTS": 256, "CS": 256,
    "SVX": (5, 128), "VAL": 256, "H1": 256, "H2": 256})
_declare("sbuf", F16, {"CC": 256, "SELF": 128, "OPC": 256, "MH": 128 * len(MATH)})
_declare("sbuf", I32, {
    "IOTA": 4096, "LG": (16, 16), "LA": (16, 16), "LBM": (16, 16), "LT": (16, 16), "THI": 512, "PM": 128, "PR": 128,
    "MC": 128, "TMPA": 128, "TMPB": 128, "C16": 16, "P15": 16, "PI": 256, "SH": 256, "S1": 256, "NHT": 256, "AH": 256,
    "BH": 256, "AB_0": 256, "AS": 1280, "SVI": 80, "SVH": (5, 16), "SVL": (5, 16)})
_declare("sbuf", F32, {
    "DUMP": 16, "MF": 128 * len(MATF), "TS": 256, "DXS": 256, "DGN": 256, "MN": 128,
    "MNG": 128, "MNA": 128, "G0": 256, "GN": 256, "FN": 128, "TR": 112, "GL": 16, "NMG": 128, "OPAF": 256, "OPBF": 256,
    "TKN": 128, "VALF": 256, "A1": 128, "Q1": 16, "Q2": 16, "WO": 16, "OG": (16, 16), "OA": (16, 16), "OB": (16, 16)})
_declare("sbuf", U16, {"SELU": 128, "NU": 128, "GLU": 16, "GR": 256, "OFU": 32, "WOU": 16, "GU0": 256, "GS": 1024})
PSUM = ["PV", "PL", "PG", "PN", "PT", "PM1", "PX", "VB2"]
_declare("psum", F32, {b: 512 for b in PSUM})
for _t in range(1, VIS):
    _declare("sbuf", U16, {"GU%d" % _t: 256})
    _declare("sbuf", I32, {"AB_%d" % _t: 256})
    _declare("sbuf", BF, {"CR%d" % _t: 64})
for _t in range(1, VIS - 1):
    _declare("sbuf", BF, {"VT%d" % _t: 256, "TH%d" % _t: 512, "SV%d" % _t: 128})
SEMAPHORES = (["qV", "qS", "qT", "qG", "lsem", "dx", "dxl", "dg", "da", "db", "dth", "dy", "do1", "do2", "do3", "do4"]
              + [n + "%d" % t for t in range(1, VIS) for n in ("ag", "ab", "ac")]
              + [n + "%d" % t for t in range(1, VIS - 1) for n in ("av", "at", "as")])


def rank_program(g, core, T, topo):
    rank = T.rank_of(core)
    if rank is None:
        return
    eng = {"V": g.vector, "S": g.scalar, "T": g.tensor, "G": g, "Y": g.sync}
    known = {q: {} for q in eng}
    total = {}
    clk = {}
    log = {}

    def take(q, tok):
        k = known[q]
        if k.get(tok[0], 0) >= tok[1]:
            return
        eng[q].wait_ge(T.sem[tok[0]], tok[1])
        for s, n in clk.get(tok, {}).items():
            if k.get(s, 0) < n:
                k[s] = n
        k[tok[0]] = tok[1]

    def order(q, reads, writes, dma=False):
        need = []
        for w, regs in ((False, reads), (True, writes)):
            for (b, a, e) in regs:
                ps = b in PSUM
                for (a2, e2, w2, q2, tok) in log.get(b, []):
                    over = a < e2 and a2 < e
                    same = q2 == q and not dma
                    if ps and not same:
                        need.append(tok)
                    elif over and (w or w2):
                        if same and not w2:
                            continue
                        if same and w and q == "T":
                            continue
                        need.append(tok)
        need.sort(key=lambda x: -x[1])
        for tok in need:
            take(q, tok)

    def note(q, reads, writes, tok):
        for (b, a, e) in writes:
            log[b] = [x for x in log.get(b, []) if not (a <= x[0] and x[1] <= e)] + [(a, e, True, q, tok)]
        for (b, a, e) in reads:
            log[b] = [x for x in log.get(b, []) if not (a <= x[0] and x[1] <= e and not x[2] and x[3] == q)] + [(a, e, False, q, tok)]

    def op(q, call, reads, writes):
        order(q, reads, writes)
        s = "q" + q
        total[s] = total.get(s, 0) + 1
        call().then_inc(T.sem[s], 1)
        tok = (s, total[s])
        clk[tok] = dict(known[q])
        note(q, reads, writes, tok)

    def dmas(q, sem, items):
        n = 16 * len(items)
        total[sem] = n
        tok = (sem, n)
        for (o, i, reads, writes) in items:
            order(q, reads, writes, True)
            eng[q].dma_start(o, i).then_inc(T.sem[sem], 16)
        clk[tok] = dict(known[q])
        for (o, i, reads, writes) in items:
            note("dma" + sem, reads, writes, tok)

    def W(b, a=0, n=None):
        if b in ALIAS:
            return ALIAS[b]
        return (b, a, a + (n if n is not None else int(np.prod(SCRATCH[b][1][1:])) - a))

    def R(r):
        b, a, e = r
        if b == "SVX":
            return T.SVX[:, a // 128, a % 128:a % 128 + e - a]
        return T[b][:, a:e]

    def tt(o, a, b, f):
        op("V", lambda: g.vector.tensor_tensor(R(o), R(a), R(b), f), [a, b], [o])

    def ts(o, a, s1, f1, s2=None, f2=None):
        if f2 is None:
            op("V", lambda: g.vector.tensor_scalar(R(o), R(a), s1, None, f1), [a], [o])
        else:
            op("V", lambda: g.vector.tensor_scalar(R(o), R(a), s1, s2, f1, f2), [a], [o])

    def cp(o, a):
        op("V", lambda: g.vector.tensor_copy(R(o), R(a)), [a], [o])

    def act(o, a, scale=1.0, bias=0.0):
        op("S", lambda: g.scalar.activation(R(o), R(a), Fn.Identity, bias=bias, scale=scale), [a], [o])

    def mms(o_all, items, start, stop):
        reads = []
        for (o, l, r) in items:
            reads += [l, r[0] if len(r) == 2 else r]

        def call():
            last = None
            for k, (o, l, r) in enumerate(items):
                if len(r) == 2:
                    (b, a, e), s = r
                    rhs = T[b][:, a + s:e:16]
                else:
                    rhs = R(r)
                last = g.tensor.matmul(R(o), R(l), rhs, start and k == 0, stop and k == len(items) - 1)
            return last
        op("T", call, list(dict.fromkeys(reads)), [o_all])

    mat = lambda b, s=0: (b, 128 * s, 128 * s + 128)
    nxt = {0: [(0, 128, 128)], 128: [(0, 16, 112), (112, 0, 16)]}
    prv = {128: [(0, 0, 128)], 0: [(0, 240, 16), (16, 128, 112)]}

    def send(dst, out, src, sem):
        c = T.cores[dst]
        order("G", [src], [])
        rid, pid = topo.addr(c)[:2]
        g.remote_dma(R(out), R(src), T.sem[sem], T.sem.lsem, pid, rid, topo.mask(core, c))
        total["lsem"] = total.get("lsem", 0) + len(topo.engines(core, c))

    def arrives(frm, out, sem):
        n = len(topo.engines(T.cores[frm], core))
        total[sem] = n
        note("remote", [], [out], (sem, n))

    dmas("Y", "dg", [(T.LG[:], T.gl[:], [], [W("LG")])])
    dmas("S", "dx", [(T.TAB[:, 0:4096], T.xt[:], [], [W("TAB", 0, 4096)])])
    dmas("Y", "dy", [(T.YV[:], T.yv[:], [], [W("YV")])])
    dmas("Y", "dth", [(T.LT[:], T.th[:], [], [W("LT")])])
    dmas("Y", "da", [(T.LA[:], T.al[:], [], [W("LA")])])
    dmas("Y", "db", [(T.LBM[:], T.bl[:], [], [W("LBM")])])
    dmas("Y", "dxl", [(T.XLAST[:], T.xt[:, 4080:4096], [], [W("XLAST")])])
    for t in range(1, VIS - 1):
        for b, sem in (("VT", "av"), ("TH", "at"), ("SV", "as")):
            arrives((rank - t) % 4, W("%s%d" % (b, t)), "%s%d" % (sem, t))
    for t in range(1, VIS):
        for b, sem in (("GU%d", "ag"), ("AB_%d", "ab"), ("CR%d", "ac")):
            arrives((rank - 1) % 4, W(b % t), "%s%d" % (sem, t))
    home = lambda t: t in (0, VIS - 1)
    view = lambda t: W("YV", 256 * t, 256) if home(t) else W("VT%d" % t)

    def iota(b, pat, base, cm):
        op("G", lambda: g.iota(T[b][:], pat, base, cm), [], [W(b)])
    iota("PM", [[-1, 128]], 128, 1)
    iota("PR", [[0, 128]], 0, 1)
    iota("MC", [[1, 128]], 0, 0)
    iota("C16", [[16, 16]], 0, 0)
    for b, c in ((W("SELN"), 0.0), (W("ONES"), 1.0), (W("ZER"), 0.0)):
        op("V", lambda b=b, c=c: g.vector.memset(R(b), c), [], [b])
    act(W("SEL2"), W("SELN"), 0.0)
    act(W("DS"), W("SELN"), 0.0)
    ts(W("TMPA"), W("PR"), 4, Op.arith_shift_right)
    ts(W("TMPB"), W("MC"), 4, Op.arith_shift_right)
    tt(W("BLK"), W("TMPA"), W("TMPB"), Op.is_equal)
    blk = ALIAS["BLK"][1]
    for d in (MATH, WEIGHT, MATF):
        for b, c in d.items():
            ts(W(b), W("PM"), 128.0, Op.is_equal, c, Op.mult)
    for s in range(16):
        z = (slice(None), slice(128 * s + s, 128 * s + 128, 16))
        f = (slice(None), slice(blk + s, blk + 128, 16))
        op("V", lambda z=z, f=f: g.vector.tensor_scalar(T.SELN[z], T.MAT[f], -1.0, None, Op.mult), [W("BLK")], [mat("SELN", s)])
        op("S", lambda z=z, f=f: g.scalar.activation(T.SEL2[z], T.MAT[f], Fn.Identity, bias=0.0, scale=2.0), [W("BLK")], [mat("SEL2", s)])
    for s in range(16):
        op("S", lambda s=s: g.scalar.activation(T.DS[:, 128 * s + s:128 * s + 128:16], T.MAT[:, s:128:16], Fn.Copy), [W("ID")], [mat("DS", s)])
    act(("TAB", 4095, 4096), ("ONES", 0, 1), 1024.0)

    ev = [(0, 0), (1, 128)]
    for p, c in ev:
        op("V", lambda p=p, c=c: g.vector.tensor_copy(T.GU0[:, c:c + 128], T.LG[:, p::2, :]), [W("LG")], [("GU0", c, c + 128)])
    for t in range(1, VIS - 1):
        send((rank + t) % 4, W("VT%d" % t), W("YV", 256 * t, 256), "av%d" % t)
    iota("IOTA", [[1, 4096]], 0, 0)
    for p, c in ev:
        op("V", lambda p=p, c=c: g.vector.tensor_scalar(T.THI[:, c:c + 128], T.LT[:, p::2, :], 15, None, Op.bitwise_and), [W("LT")], [("THI", c, c + 128)])
        op("V", lambda p=p, c=c: g.vector.tensor_scalar(T.THI[:, 256 + c:384 + c], T.LT[:, p::2, :], 4, None, Op.arith_shift_right), [W("LT")], [("THI", 256 + c, 384 + c)])
    cp(W("TH"), W("THI"))
    mms(("PN", 0, 80), [(("PN", 0, 80), mat("SELN", s), (W("YV"), s)) for s in range(16)], True, True)
    ts(W("SVI"), ("PN", 0, 80), -1.0, Op.mult)
    op("V", lambda: g.vector.tensor_scalar(T.SVH[:], T.SVI[:], 4, None, Op.arith_shift_right), [W("SVI")], [W("SVH")])
    op("V", lambda: g.vector.tensor_scalar(T.SVL[:], T.SVI[:], 15, None, Op.bitwise_and), [W("SVI")], [W("SVL")])
    for r in range(4):
        for b, c in (("SVH", 16 * r), ("SVL", 64 + 16 * r)):
            op("V", lambda b=b, c=c: g.vector.tensor_copy(T.SVX[:, :, c:c + 16], T[b][:]), [W(b)], [W("SVX")])
    for t in range(1, VIS - 1):
        send((rank + t) % 4, W("TH%d" % t), W("TH"), "at%d" % t)
        send((rank + t) % 4, W("SV%d" % t), W("SVX", 128 * t, 128), "as%d" % t)

    def late():
        for p, c in ev:
            op("V", lambda p=p, c=c: g.vector.tensor_scalar(T.G0[:, c:c + 128], T.LA[:, p::2, :], -4096.0, 4095.0 * 4096 + 4095, Op.mult, Op.add), [W("LA")], [("G0", c, c + 128)])
            op("V", lambda p=p, c=c: g.vector.tensor_copy(T.GN[:, c:c + 128], T.LBM[:, p::2, :]), [W("LBM")], [("GN", c, c + 128)])
        tt(W("AB_0"), W("G0"), W("GN"), Op.subtract)

    def later():
        ts(W("TMPA"), W("PM"), 15, Op.bitwise_and)
        ts(W("MOD16"), W("TMPA"), 0.0, Op.is_equal)
        ts(W("TMPC"), W("PM"), 128.0, Op.is_lt)
        tt(W("TRI"), W("TMPC"), W("BLK"), Op.mult)
        for e in range(8):
            ts(mat("WE", e), W("ID"), 256.0 * e, Op.mult)
        ts(W("P15"), ("PR", 0, 16), 15, Op.bitwise_and)
        tt(W("IDX"), W("C16"), W("P15"), Op.add)
        ts(W("DUMP"), W("IDX"), 4096.0, Op.add)

    def prepare(t):
        for h in (0, 256):
            mms(W("PV"), [(("PV", h, h + 256), W("ID"), view(t))], True, True)

    def visit(t):
        M = 0 if t % 2 == 0 else 128
        O = 128 - M
        hm = lambda b: (b, M, M + 128)
        ho = lambda b: (b, O, O + 128)
        gu = W("GU%d" % t)
        ab = W("AB_%d" % t)
        last = t == VIS - 1
        ones = ("ONES", 0, 128)

        def gather(out, c, lst, lc):
            op("S", lambda: g.scalar.activation(T[out][:, 1024 * c:1024 * c + 1024], T.TAB[:, 0:4096].indirect(T[lst][:, lc:lc + 64]), Fn.Copy),
               [W("TAB", 0, 4096), (lst, lc, lc + 64)], [(out, 1024 * c, 1024 * c + 1024)])

        def maxes(x, c, n):
            for h in range(2):
                a, z = 1024 * c + 512 * h, 1024 * n + 512 * h
                tt(("MX", z, z + 512), (x, a, a + 512), W("PV"), Op.max)

        def sumx(x, c, bank, col, extra=()):
            out = (bank, col, col + 64)
            mms(out, [(out, mat("SELN", s), ((x, 1024 * c, 1024 * c + 1024), s)) for s in range(16)] + [(out, l, r) for l, r in extra], True, False)

        def sum2(n, bank, col):
            out = (bank, col, col + 64)
            mms(out, [(out, mat("SEL2", s), (("MX", 1024 * n, 1024 * n + 1024), s)) for s in range(16)], False, True)

        gather("XRM", 0, gu[0], M)
        gather("XRM", 1, gu[0], M + 64)
        ts(W("CC"), gu, -2048.0, Op.add)
        r = ("PL", 0, 256)
        mms(r, [(r, W("NID"), W("ONES")), (r, W("M101"), W("CC"))]
            + [(("PL", b + d, b + d + n), W("M65"), ("CC", s, s + n)) for b in (0, 128) for d, s, n in nxt[b]], True, True)
        ts(W("FB"), gu, 4095.0, Op.is_lt)
        r = ("PL", 256, 384)
        mms(r, [(r, W("P4K"), ho("FB")), (r, W("P2K"), ones), (r, W("NID"), ones)], True, True)
        for b in (0, 128):
            for d, s, n in nxt[b]:
                tt(("PI", b + d, b + d + n), ("CC", b + d, b + d + n), ("CC", s, s + n), Op.mult)
        ts(W("SH"), W("PI"), 5, Op.arith_shift_right)
        tt(W("S1"), ("PL", 0, 256), W("SH"), Op.subtract)
        ts(W("NHT"), W("S1"), 4095, Op.bitwise_and)
        tt(("VB2", 0, 128), ("PL", 256, 384), ho("NHT"), Op.subtract)
        ts(W("NU"), hm("NHT"), -1.0, Op.mult, 4095.0, Op.add)
        tt(W("SELF"), ("VB2", 0, 128), ho("CC"), Op.min)
        ts(hm("HE2"), hm("FB"), -2 * H, Op.mult, 2 * H, Op.add)
        ts(W("SELU"), W("SELF"), 2048.0, Op.add)
        th, sv, z = ("TH", "SVX", 128 * t) if home(t) else ("TH%d" % t, "SV%d" % t, 0)
        r = ("PT", 0, 256)
        mms(r, [(r, W("NID"), (th, 0, 256)), (r, W("N16"), (th, 256, 512))]
            + [(("PT", h, h + 64), W(m), (sv, z + c, z + c + 64)) for h in range(0, 256, 64) for m, c in (("N16", 0), ("NID", 64))], True, False)
        px = ("PX", 0, 256)
        mms(px, [(px, W("P2K"), W("ONES")), (px, W("NID"), W("ONES")), (px, W("NIDH"), W("CC"))], True, False)
        if t == 0:
            later()
        gather("XRO", 0, "SELU", 0)
        gather("XRO", 1, "SELU", 64)
        maxes("XRM", 0, 0)
        sumx("XRM", 0, "PG", M)
        sum2(0, "PG", M)
        maxes("XRM", 1, 1)
        sumx("XRM", 1, "PG", M + 64)
        sum2(1, "PG", M + 64)
        if t == 0:
            late()
        gather("XRN", 0, "NU", 0)
        maxes("XRO", 0, 2)
        sumx("XRO", 0, "PG", O, [(W("PH"), ("FB", O, O + 64))])
        sum2(2, "PG", O)
        ts(W("EA"), ab, 4096.0, Op.is_lt)
        r = ("PT", 0, 256)
        mms(r, ([(("PT", h, h + 64), W("NID"), W("CR%d" % t)) for h in range(0, 256, 64)] if t > 0 else [])
            + [(r, W("PH"), W("FB")), (("PT", O, O + 128), W("NH"), ones)]
            + [(("PT", b + d, b + d + n), W("NH"), ("FB", s, s + n)) for b in (0, 128) for d, s, n in nxt[b]]
            + [(r, W("NH"), W("EA"))], False, True)
        ts(W("AH"), ab, 12, Op.arith_shift_right)
        ts(W("BH"), ab, 4095, Op.bitwise_and)
        maxes("XRO", 1, 3)
        sumx("XRO", 1, "PG", O + 64, [(W("PH"), ("FB", O + 64, O + 128))])
        sum2(3, "PG", O + 64)
        act(W("TS"), ("PT", 0, 256), -1.0, H)
        act(ho("DXS"), ho("PG"), 1.0, -H)
        gather("XRN", 1, "NU", 64)
        maxes("XRN", 0, 4)
        sumx("XRN", 0, "PN", 0)
        sum2(4, "PN", 0)
        tt(W("OPB"), ("PG", 0, 256), W("TS"), Op.is_gt)
        r = ("PM1", 256, 512)
        mms(r, [(r, W("ID"), W("OPB"))], True, True)
        mms(px, [(px, W("N2K"), W("OPB")), (px, W("ID"), W("OPB"))], False, False)
        r = ("PL", 0, 128)
        mms(r, [(r, W("PH"), hm("FB")), (r, W("NH"), ones)] + [(("PL", d, d + n), W("NH"), ("OPB", s, s + n)) for d, s, n in nxt[M]], True, True)
        r = ("PL", 128, 256)
        mms(r, [(r, W("NH"), hm("FB"))] + [(("PL", 128 + d, 128 + d + n), W("NH"), ("OPB", s, s + n)) for d, s, n in prv[M]], True, True)
        tt(hm("DGN"), hm("PG"), hm("HE2"), Op.subtract)
        for d, s, n in nxt[M]:
            tt(("MN", d, d + n), ("PG", M + d, M + d + n), ("DXS", s, s + n), Op.min)
        for d, s, n in nxt[O]:
            tt(("VB2", d, d + n), ("PG", O + d, O + d + n), ("DGN", s, s + n), Op.is_lt)
        tt(W("OPAF"), ("PM1", 256, 512), W("AH"), Op.mult)
        mms(px, [(px, W("I1F"), W("OPAF"))], False, False)
        tt(W("OPBF"), ("PM1", 256, 512), W("BH"), Op.mult)
        mms(px, [(("PX", b + d, b + d + n), W("I1F"), ("OPBF", s, s + n)) for b in (0, 128) for d, s, n in prv[b]], False, False)
        for d, s, n in prv[O]:
            tt(("TKO", d, d + n), ("VB2", d, d + n), ("OPB", s, s + n), Op.is_gt)
        tt(W("OPC"), ("PM1", 256, 512), W("CC"), Op.mult)
        tt(W("TKN"), W("TKO"), ho("NHT"), Op.mult)
        sumx("XRN", 1, "PN", 64)
        mms(px, [(px, W("PIDH"), W("OPC"))], False, False)
        mms(px, [(("PX", O, O + 128), W("I1F"), W("TKN"))], False, True)
        tt(W("MNG"), ("PL", 0, 128), W("MN"), Op.add)
        tt(("VB2", 128, 256), ("PL", 128, 256), W("MN"), Op.add)
        maxes("XRN", 1, 5)
        sum2(5, "PN", 64)
        tt(W("MNA"), ("VB2", 128, 256), W("MNG"), Op.max)
        gx = ("PX", M, M + 128)
        tt(("VB2", 256, 384), gx, hm("NHT"), Op.subtract)
        tt(W("MGB"), ("PN", 0, 128), W("MNG"), Op.is_lt)
        r = ("PM1", 0, 128)
        mms(r, [(r, W("N16"), W("MGB"))] + [(("PM1", 16 * d, 128), W("ID"), ("MGB", 0, 128 - 16 * d)) for d in range(1, 8)], True, True)
        tt(W("MTB"), ("PN", 0, 128), W("MNA"), Op.is_lt)
        tt(W("NMG"), ("PN", 0, 128), W("MNG"), Op.is_ge)
        if not last:
            r = ("PT", 0, 16)
            mms(r, [(r, W("MOD16"), ("MGB", 16 * e, 16 * e + 16)) for e in range(8)], True, True)
            for k in range(4):
                act(W("CS", 64 * t + 16 * k, 16), r)

        def places():
            tt(hm("G0"), ("VB2", 256, 384), W("MTB"), Op.mult)
            for d, s, n in prv[O]:
                tt(("GN", O + d, O + d + n), ("PX", O + d, O + d + n), ("NMG", s - M, s - M + n), Op.mult)
            tt(hm("GN"), gx, hm("G0"), Op.subtract)

        def memories():
            z = 256 * t
            tt(("AS", z + O, z + O + 128), ("PL", 256 + O, 384 + O), ho(ab[0]), Op.mult)
            tt(("VB2", 384, 512), ("PL", 256 + M, 384 + M), hm(ab[0]), Op.mult)
            tt(W("A1"), ("PX", 256, 384), W("MGB"), Op.mult)
            tt(("AS", z + M, z + M + 128), ("VB2", 384, 512), W("A1"), Op.add)
            if not last:
                send((rank + 1) % 4, W("AB_%d" % (t + 1)), W("AS", z, 256), "ab%d" % (t + 1))

        if not last:
            places()
            ts(W("GS", 256 * t, 256), W("GN"), -1.0, Op.mult, 4095.0, Op.add)
            send((rank + 1) % 4, W("GU%d" % (t + 1)), W("GS", 256 * t, 256), "ag%d" % (t + 1))
            send((rank + 1) % 4, W("CR%d" % (t + 1)), W("CS", 64 * t, 64), "ac%d" % (t + 1))
        kp = ("PL", 256, 512)
        mms(kp, [(kp, W("ID"), W("ONES")), (kp, W("NID"), W("OPB"))]
            + [(("PL", 256 + b + d, 256 + b + d + n), W("NID"), ("OPB", s, s + n)) for b in (0, 128) for d, s, n in prv[b]]
            + [(("PL", 256 + O, 384 + O), W("NID"), W("TKO")), (("PL", 256 + M, 384 + M), W("NID"), W("MTB"))]
            + [(("PL", 256 + O + d, 256 + O + d + n), W("NID"), ("MGB", s - M, s - M + n)) for d, s, n in prv[O]], True, True)
        ts(W("FMB"), ("PM1", 0, 128), -16.0, Op.is_equal)
        sh = t % 2
        for k in range(1 + sh):
            r = ("PM1", 128 + 16 * k, 144 + 16 * k)
            mms(r, [(r, W("ID"), W("IDX"))] + [(r, mat("WE", (e + k) % 8), ("FMB", 16 * e, 16 * e + 16)) for e in range(8)], True, True)
        pt = ("PT", 256, 512)
        mms(pt, [(pt, W("ZER"), W("ONES"))], True, False)

        def both():
            r = ("PX", 256, 384)
            mms(r, [(r, W("P8M"), ones), (r, W("N2K"), ones), (r, W("NID"), ones), (r, W("N4KH"), hm("CC"))]
                + [(("PX", 256 + d, 256 + d + n), W("NIDH"), ("CC", s, s + n)) for d, s, n in nxt[M]], True, True)
        if not last:
            both()
        tt(W("FN"), W("FMB"), hm("NHT"), Op.mult)
        tt(("TR", 0, 64), ("FN", 0, 64), ("FN", 64, 128), Op.add)
        tt(("TR", 64, 96), ("TR", 0, 32), ("TR", 32, 64), Op.add)
        tt(("TR", 96, 112), ("TR", 64, 80), ("TR", 80, 96), Op.add)
        ts(W("GLU"), ("TR", 96, 112), -1.0, Op.mult, 4095.0, Op.add)
        ts(W("GL"), ("TR", 96, 112), -1.0, Op.mult, 4095.0, Op.add)
        op("V", lambda: g.vector.tensor_copy(T.GR[:], T.IOTA[:].indirect(T.GLU[:])), [W("IOTA"), W("GLU")], [W("GR")])
        cp(("OFU", 0, 16 + 16 * sh), ("PM1", 128, 144 + 16 * sh))
        for h, x, c in (("H1", "XRM", 0), ("H2", "XRO", 16 * sh)):
            op("S", lambda h=h, x=x, c=c: g.scalar.activation(T[h][:], T[x][:].indirect(T.OFU[:, c:c + 16]), Fn.Copy), [W(x), ("OFU", c, c + 16)], [W(h)])
        at = 0
        for c in range(16):
            n = 256 - 16 * c
            op("V", lambda c=c, at=at, n=n: g.vector.tensor_scalar(T.EQ[:, at:at + n], T.GR[:, 16 * c:256], T.GL[:, c:c + 1], None, Op.is_equal),
               [W("GR"), W("GL")], [("EQ", at, at + n)])
            it = [(("PT", 256 + 16 * c, 272 + 16 * c), W("TRI"), ("EQ", at, at + 16))]
            if n > 16:
                it.append((("PT", 272 + 16 * c, 512), W("BLK"), ("EQ", at + 16, at + n)))
            mms(pt, it, False, c == 15)
            at += n
        ts(W("NOM"), ("TR", 96, 112), 0.0, Op.is_equal)
        cp(W("OUTS"), pt)
        nm = ("PN", 256, 512)
        mms(nm, [(nm, W("HALF"), W("H1")), (nm, W("HALF"), W("H2")), (nm, W("N25"), W("ONES"))], True, True)
        r = ("PM1", 160, 176)
        mms(r, [(r, W("ID"), W("NOM"))] + [(r, mat("DS", s), (W("OUTS"), s)) for s in range(16)], True, True)
        act(W("VALF"), nm, 1.0, BIG)
        act(W("VAL"), W("VALF"), 1.0, -BIG)
        if not last:
            prepare(t + 1)
            memories()
        ts(W("Q1"), r, 0.0, Op.is_gt)
        tt(W("Q2"), W("Q1"), W("DUMP"), Op.mult)
        tt(W("WO"), W("Q2"), W("GL"), Op.max)
        cp(W("WOU"), W("WO"))
        op("V", lambda: g.vector.tensor_copy(T.TAB[:].indirect(T.WOU[:]), T.VAL[:]), [W("VAL"), W("WOU")], [W("TAB")])
        if last:
            cp(("TAB", 4095, 4096), ("XLAST", 15, 16))
            dmas("S", "do4", [(T.ox[:], T.TAB[:, 0:4096], [W("TAB", 0, 4096)], [])])
            places()
            both()
            memories()

    prepare(0)
    for t in range(VIS):
        visit(t)

    def put(dst, src, sem, out):
        for p, c in ev:
            op("V", lambda p=p, c=c: g.vector.tensor_scalar(T[dst][:, p::2, :], T[src][:, c:c + 128], -1.0, 4095.0, Op.mult, Op.add),
               [(src, c, c + 128)], [(dst, c, c + 128)])
        dmas("Y", sem, [(T[out][:], T[dst][:], [W(dst)], [])])
    put("OG", "GN", "do1", "og")
    new = W("AS", 256 * (VIS - 1), 256)
    ts(W("AH"), new, 12, Op.arith_shift_right)
    put("OA", "AH", "do2", "oa")
    ts(W("BH"), new, 4095, Op.bitwise_and)
    put("OB", "BH", "do3", "ob")
    for s in total:
        take("G", (s, total[s]))
